import numpy as np
import ml_dtypes


def mxq(x, axis, fmt="e4m3"):
    dtype, down = {"e4m3": (ml_dtypes.float8_e4m3fn, 7), "e5m2": (ml_dtypes.float8_e5m2, 14)}[fmt]
    v = np.moveaxis(np.asarray(x, np.float32).astype(ml_dtypes.bfloat16).astype(np.float64), axis, -1)
    blocks = v.reshape(v.shape[:-1] + (-1, 32))
    amax = np.abs(blocks).max(-1, keepdims=True)
    byte = np.maximum(np.where(amax > 0, np.frexp(amax)[1] - 1 + 127, 0) - down, 1)
    scale = np.exp2(byte - 127.0)
    codes = (blocks / scale).astype(np.float32).astype(dtype).astype(np.float64)
    return np.moveaxis((codes * scale).reshape(v.shape), -1, axis)


WIDE = False


def mx_kscale(k):
    if not WIDE:
        return np.ones(k)
    levels = np.array([10, -10, 5, -5, 0])
    if k % 512:
        return np.exp2(np.random.permutation(np.resize(levels, k // 32))).repeat(32)
    a = np.empty((k // 512, 16))
    for p in range(k // 512):
        a[p, :8] = np.random.permutation(np.resize(levels, 8))
        for g in range(8):
            far = levels[np.abs(levels - a[p, g]) >= 10]
            a[p, g + 8] = far[np.random.randint(len(far))]
    return np.exp2(a.ravel()).repeat(32)


BF16 = ml_dtypes.bfloat16


def bf(x):
    return np.asarray(x, np.float32).astype(BF16)


def f64(x):
    return np.asarray(x).astype(np.float64)


E2M1 = np.array([0.0, 0.5, 1.0, 1.5, 2.0, 3.0, 4.0, 6.0, -0.0, -0.5, -1.0, -1.5, -2.0, -3.0, -4.0, -6.0])


def pack_weight(w, fmt):
    k, n = w.shape
    w = f64(bf(w)).reshape(k // 32, 32, n)
    amax = np.abs(w).max(1)
    if fmt == "e4m3":
        byte = np.frexp(amax)[1] - 1 + 127 - 7
    else:
        mant, ex = np.frexp(amax / 6.0)
        byte = np.where(mant > 0.5, ex, ex - 1) + 127
    byte = np.clip(np.where(amax > 0, byte, 1), 1, 254)
    scaled = (w * np.exp2(127.0 - byte)[:, None, :]).reshape(k, n).astype(np.float32)
    by_word = np.ascontiguousarray(scaled.reshape(k // 512, 128, 4, n).transpose(0, 1, 3, 2))
    if fmt == "e4m3":
        words = by_word.astype(ml_dtypes.float8_e4m3fn).view(np.uint8)
    else:
        c = by_word.astype(ml_dtypes.float4_e2m1fn).view(np.uint8) & 0xF
        words = c[..., 0::2] | (c[..., 1::2] << 4)
    return np.ascontiguousarray(words), np.ascontiguousarray(byte.astype(np.uint8).reshape(k // 512, 16, n))


def unpack_weight(words, scales, fmt):
    g, p, n, _ = words.shape
    if fmt == "e4m3":
        vals = np.ascontiguousarray(words).view(ml_dtypes.float8_e4m3fn).astype(np.float64)
    else:
        nib = np.empty((g, p, n, 4), np.uint8)
        nib[..., 0::2] = words & 0xF
        nib[..., 1::2] = words >> 4
        vals = E2M1[nib]
    vals = vals * np.repeat(np.exp2(scales.astype(np.float64) - 127.0), 8, axis=1)[..., None]
    return vals.transpose(0, 1, 3, 2).reshape(g * 512, n)
def pack4(w):
    words, scales = pack_weight(w, "e2m1")
    return words.reshape(words.shape[0], 128, -1), scales


def unpack4(words, scales):
    return unpack_weight(words.reshape(words.shape[0], 128, -1, 2), scales, "e2m1")


def planes(Y):
    n, m = Y.shape
    b = f64(bf(Y)).reshape(n // 32, 32, m)
    amax = np.abs(b).max(1)
    byte = np.clip(np.where(amax > 0, np.frexp(amax)[1] - 1 + 127 - 7, 1), 1, 254)
    codes = (b * np.exp2(127.0 - byte)[:, None, :]).reshape(n, m).astype(np.float32).astype(ml_dtypes.float8_e4m3fn).view(np.uint8)
    words = codes.reshape(n // 512, 128, 4, m).transpose(0, 1, 3, 2)
    return np.ascontiguousarray(words), np.ascontiguousarray(byte.astype(np.uint8).reshape(n // 512, 16, m))


Q, C, P, T = 1024, 512, 4096, 512

def setup_inputs():
    s = mx_kscale(C)
    t = mx_kscale(P)
    u = np.random.randn(P)
    v = 0.7 * np.random.randn(C)
    k = 2.0 * np.random.randn(T)
    F = 0.5 + v[:, None] * u + np.random.randn(C, P)
    E = 1.5 * np.random.randn(C, Q) / np.sqrt(C) - 3.0 / C
    query_words, query_scales = pack4(E * s[:, None])
    pixel_words, pixel_scales = pack4(F / s[:, None])
    w = np.exp(0.5 * np.random.randn(P)) / np.sqrt(P)
    logits = u[:, None] * k + 1.5 * np.random.randn(P, T) - 1.0 + np.random.randn(T)
    masks = 1.0 / (1.0 + np.exp(-logits))
    masks[:, -1] = 1.0
    area = (w[:, None] * masks).sum(axis=0)
    return {"query_words": query_words, "query_scales": query_scales,
            "pixel_words": pixel_words, "pixel_scales": pixel_scales,
            "pixel_weight": bf(w * t), "target_masks": bf(masks / t[:, None]),
            "target_area": bf(area), "target_gain": bf(2.0 * np.exp(0.8 * np.random.randn(T)))}

def reference(query_words, query_scales, pixel_words, pixel_scales, pixel_weight, target_masks, target_area, target_gain):
    E = unpack4(query_words, query_scales)
    F = unpack4(pixel_words, pixel_scales)
    L = E.T @ F
    H = f64(pixel_weight) / (1.0 + np.exp(-L))
    I = mxq(H, 1) @ mxq(f64(target_masks), 0)
    D = I[:, -1:] + f64(target_area)
    y = f64(target_gain) * I / D
    words, scales = planes(y.T)
    return y, words, scales

@@ -1,0 +1,422 @@
+from contextlib import ExitStack
+
+import concourse.mybir as mybir
+from concourse.masks import make_identity
+
+QUERIES, CHANNELS, PIXELS, TARGETS = 1024, 512, 4096, 512
+FLOPS = 2 * QUERIES * PIXELS * (CHANNELS + TARGETS)
+
+F32 = mybir.dt.float32
+BF16 = mybir.dt.bfloat16
+I32 = mybir.dt.int32
+U32 = mybir.dt.uint32
+U8 = mybir.dt.uint8
+FP8X4 = mybir.dt.float8_e4m3fn_x4
+FP4X4 = mybir.dt.float4_e2m1fn_x4
+ACT = mybir.ActivationFunctionType
+ALU = mybir.AluOpType
+
+P = 128
+SLOTS = 4
+K_PASS = P * SLOTS
+PASSES = PIXELS // K_PASS
+HALF = 512
+HALVES = QUERIES // HALF
+STEPS = HALVES * PASSES
+F_CHUNKS = ((0, 2), (2, 5), (5, 8))
+FIRST = F_CHUNKS[0][1] * K_PASS
+SIG_RING = 4
+LEAD = 2
+LAG = 3
+H_RING = 2
+T_RING = 2
+POOL_SLOTS = 3
+OUT_RING = 4
+
+
+def tile_mask_dice_matching_k5_kernel(
+    tc, query_words, query_scales, pixel_words, pixel_scales, pixel_weight,
+    target_masks, target_area, target_gain, out_0, out_1, out_2,
+):
+    nc = tc.nc
+    with ExitStack() as ctx:
+        sb = ctx.enter_context(tc.tile_pool(name="sb", bufs=1))
+        ps = ctx.enter_context(tc.psum_pool(name="ps", bufs=1))
+        ctx.enter_context(tc.manual_schedule())
+
+        def tiles(name, count, shape, dtype):
+            return [sb.tile(shape, dtype, name="%s%d" % (name, n), align_bytes=64) for n in range(count)]
+
+        def one(name, shape, dtype):
+            return sb.tile(shape, dtype, name=name, align_bytes=64)
+
+        e_codes = tiles("e_codes", HALVES, [P, 2 * HALF], U8)
+        e_scales = one("e_scales", [P, QUERIES], U8)
+        f_raw = [one("f_raw%d" % a, [P, (b - a) * K_PASS // 2], I32) for a, b in F_CHUNKS]
+        f_scales_first = one("f_scales_first", [P, FIRST], U8)
+        f_scales_rest = one("f_scales_rest", [P, PIXELS - FIRST], U8)
+        f_codes = [one("f_codes%d" % a, [P, (b - a) * K_PASS * 2], U8) for a, b in F_CHUNKS]
+        f_scales = [one("f_scales%d" % a, [P, (b - a) * K_PASS], U8) for a, b in F_CHUNKS]
+        w_raw = one("w_raw", [PASSES, K_PASS], BF16)
+        w_rows = one("w_rows", [P, SLOTS, P], F32)
+        w_cols = one("w_cols", [P, PASSES * SLOTS], F32)
+        ident = one("ident", [P, P], F32)
+        consts_raw = one("consts_raw", [P, 2, 16], BF16)
+        consts = one("consts", [P, 2, SLOTS], F32)
+        warm = one("warm", [P, 8], F32)
+        warm_out = one("warm_out", [P, 8], F32)
+        t_raw = one("t_raw", [P, PASSES, SLOTS, TARGETS], BF16)
+        t_grouped = tiles("t_grouped", T_RING, [P, SLOTS * TARGETS], BF16)
+        t_codes = tiles("t_codes", PASSES, [P, TARGETS], U32)
+        t_scales = tiles("t_scales", PASSES, [P, TARGETS], U8)
+        frame_grouped = one("frame_grouped", [P, PASSES, 4, SLOTS], BF16)
+        frame_codes4 = one("frame_codes4", [P, PASSES * 4], I32)
+        frame_scales4 = one("frame_scales4", [P, PASSES * 4], U8)
+        frame_codes = one("frame_codes", [P, PASSES, P], I32)
+        frame_scales = one("frame_scales", [P, PASSES * P], U8)
+        sig = tiles("sig", SIG_RING, [P, SLOTS * HALF], F32)
+        h_grouped = tiles("h_grouped", H_RING, [P, HALF * SLOTS], BF16)
+        h_codes = tiles("h_codes", STEPS, [P, HALF], U32)
+        h_scales = tiles("h_scales", STEPS, [P, HALF], U8)
+        rsq = tiles("rsq", SLOTS, [P, HALF], F32)
+        inv = tiles("inv", SLOTS, [P, HALF], F32)
+        y_t = one("y_t", [P, SLOTS * HALF], F32)
+        y_grouped = one("y_grouped", [P, HALF * SLOTS], BF16)
+        y_codes = tiles("y_codes", HALVES, [P, HALF], U32)
+        y_scales = one("y_scales", [P, QUERIES], U8)
+        y_rows = tiles("y_rows", OUT_RING, [P, TARGETS], F32)
+
+        logit_bank = [ps.tile([P, 512], F32, name="logit%d" % n) for n in range(3)]
+        w_bank = ps.tile([P, 512], F32, name="w_bank")
+        acc = [ps.tile([P, 512], F32, name="acc%d" % n) for n in range(SLOTS)]
+
+        def chunk_of(g):
+            return [n for n, (a, b) in enumerate(F_CHUNKS) if a <= g < b][0]
+
+        def load_scale_rows(queue, plane, rows, quadrant):
+            queue.dma_start(
+                out=plane[32 * quadrant : 32 * quadrant + 4, :].bitcast(I32),
+                in_=rows[4 * quadrant : 4 * quadrant + 4, :].bitcast(I32),
+            )
+
+        def load_e(h):
+            nc.sync.dma_start(out=e_codes[h][:].bitcast(I32),
+                              in_=query_words[0, :, 2 * HALF * h : 2 * HALF * (h + 1)].bitcast(I32))
+
+        def load_f(n):
+            a, b = F_CHUNKS[n]
+            nc.sync.dma_start(out=f_raw[n][:], in_=pixel_words[0, :, 2 * K_PASS * a : 2 * K_PASS * b].bitcast(I32))
+
+        t_view = target_masks.rearrange("(g a t e) c -> g e a t c", g=PASSES, t=SLOTS, e=4)
+
+        def load_t(g):
+            for e in range(4):
+                nc.sync.dma_start(out=t_raw[e:P:4, g, :, :], in_=t_view[g, e])
+
+        def deal_f(n):
+            a, b = F_CHUNKS[n]
+            raw_scales = f_scales_first[:] if n == 0 else f_scales_rest[:, K_PASS * a - FIRST : K_PASS * b - FIRST]
+            nc.vector.tensor_copy(
+                out=f_codes[n][:].bitcast(I32).rearrange("p (g t a w) -> p g t a w", t=SLOTS, a=32, w=2),
+                in_=f_raw[n][:].rearrange("p (g a t w) -> p g t a w", t=SLOTS, a=32, w=2),
+            )
+            nc.vector.tensor_copy(
+                out=f_scales[n][:].bitcast(I32).rearrange("p (g t a) -> p g t a", t=SLOTS, a=32),
+                in_=raw_scales.bitcast(I32).rearrange("p (g a t) -> p g t a", t=SLOTS, a=32),
+            )
+
+        def logits(s, t, bank):
+            h, g = divmod(s, PASSES)
+            n = chunk_of(g)
+            col = ((g - F_CHUNKS[n][0]) * SLOTS + t) * P
+            nc.tensor.matmul_mx(
+                out=bank[:],
+                lhsT=f_codes[n][:, 2 * col : 2 * (col + P)].bitcast(FP4X4),
+                lhsT_scale=f_scales[n][:, col : col + P],
+                rhs=e_codes[h][:].bitcast(FP4X4),
+                rhs_scale=e_scales[:, HALF * h : HALF * (h + 1)],
+                start=True, stop=True,
+            )
+            nc.scalar.activation(out=sig[s % SIG_RING][:, HALF * t : HALF * (t + 1)], in_=bank[:], func=ACT.Sigmoid)
+
+        def weigh(s):
+            g = s % PASSES
+            weights = w_bank if s < PASSES else w_cols
+            nc.vector.tensor_tensor(
+                out=h_grouped[s % H_RING][:].rearrange("p (c i t) -> p c t i", i=2, t=SLOTS),
+                in0=sig[s % SIG_RING][:].rearrange("p (t c i) -> p c t i", i=2, t=SLOTS),
+                in1=weights[:, SLOTS * g : SLOTS * (g + 1)].unsqueeze(1).unsqueeze(3).to_broadcast([P, HALF // 2, SLOTS, 2]),
+                op=ALU.mult,
+            )
+
+        def quantize_h(s):
+            nc.vector.quantize_mx(out=h_codes[s][:].bitcast(FP8X4), scales=h_scales[s][:], in_=h_grouped[s % H_RING][:])
+
+        def group_t_pool(g):
+            nc.gpsimd.tensor_scalar(
+                out=t_grouped[g % T_RING][:, : POOL_SLOTS * TARGETS].rearrange("p (u m j) -> p u m j", u=POOL_SLOTS, j=SLOTS),
+                in0=t_raw[:, g, :, :].rearrange("p j (m u) -> p u m j", u=SLOTS)[:, :POOL_SLOTS],
+                scalar1=1.0, scalar2=0.0, op0=ALU.mult, op1=ALU.add,
+            )
+
+        def group_t_scalar(g):
+            for u in range(POOL_SLOTS, SLOTS):
+                nc.scalar.copy(
+                    out=t_grouped[g % T_RING][:, u * TARGETS : (u + 1) * TARGETS].rearrange("p (m i j) -> p m j i", i=2, j=SLOTS),
+                    in_=t_raw[:, g, :, :].rearrange("p j (m i u) -> p u m j i", u=SLOTS, i=2)[:, u],
+                )
+
+        def quantize_t(g):
+            nc.vector.quantize_mx(out=t_codes[g][:].bitcast(FP8X4), scales=t_scales[g][:], in_=t_grouped[g % T_RING][:])
+
+        def group_frame():
+            nc.vector.tensor_copy(
+                out=frame_grouped[:],
+                in_=t_raw[:, :, :, TARGETS - 1].unsqueeze(2).to_broadcast([P, PASSES, 4, SLOTS]),
+            )
+
+        def quantize_frame():
+            nc.vector.quantize_mx(out=frame_codes4[:].bitcast(FP8X4), scales=frame_scales4[:],
+                                  in_=frame_grouped[:].rearrange("p g c j -> p (g c j)"))
+
+        def spread_frame():
+            nc.vector.tensor_copy(
+                out=frame_codes[:],
+                in_=frame_codes4[:].rearrange("p (g c) -> p g c", c=4)[:, :, 0:1].to_broadcast([P, PASSES, P]),
+            )
+            nc.vector.tensor_copy(
+                out=frame_scales[:].bitcast(I32).rearrange("p (g c) -> p g c", g=PASSES),
+                in_=frame_scales4[:].bitcast(I32).unsqueeze(2).to_broadcast([P, PASSES, P // 4]),
+            )
+
+        def intersect(s, u):
+            g = s % PASSES
+            nc.tensor.matmul_mx(
+                out=acc[u][:],
+                lhsT=t_codes[g][:, P * u : P * (u + 1)].bitcast(FP8X4),
+                lhsT_scale=t_scales[g][:, P * u : P * (u + 1)],
+                rhs=h_codes[s][:].bitcast(FP8X4), rhs_scale=h_scales[s][:],
+                start=(g == 0), stop=(g == PASSES - 1),
+            )
+
+        def predicted_area(s, bank):
+            g = s % PASSES
+            nc.tensor.matmul_mx(
+                out=bank[:],
+                lhsT=frame_codes[:, g, :].bitcast(FP8X4),
+                lhsT_scale=frame_scales[:, P * g : P * (g + 1)],
+                rhs=h_codes[s][:].bitcast(FP8X4), rhs_scale=h_scales[s][:],
+                start=(g == 0), stop=(g == PASSES - 1),
+            )
+
+        def inverse_root(u, bank):
+            nc.scalar.activation(out=rsq[u][:], in_=bank[:], func=ACT.Abs_reciprocal_sqrt, bias=consts[:, 0, u : u + 1])
+
+        def square(u):
+            nc.scalar.activation(out=inv[u][:], in_=rsq[u][:], func=ACT.Square)
+
+        def square_vector(u):
+            nc.vector.tensor_tensor(out=inv[u][:], in0=rsq[u][:], in1=rsq[u][:], op=ALU.mult)
+
+        def inverses(bank):
+            for u in range(SLOTS + 1):
+                if u < SLOTS:
+                    inverse_root(u, bank)
+                if u >= 1:
+                    square(u - 1)
+
+        def load_root_table():
+            nc.scalar.activation(out=warm_out[:], in_=ident[:, :8], func=ACT.Abs_reciprocal_sqrt, bias=1.0)
+
+        def ratio(u):
+            nc.vector.scalar_tensor_tensor(
+                out=y_t[:, HALF * u : HALF * (u + 1)], in0=acc[u][:], scalar=consts[:, 1, u : u + 1],
+                in1=inv[u][:], op0=ALU.mult, op1=ALU.mult,
+            )
+
+        def group_y():
+            nc.vector.tensor_copy(
+                out=y_grouped[:].rearrange("p (c i u) -> p c u i", i=2, u=SLOTS),
+                in_=y_t[:].rearrange("p (u c i) -> p c u i", i=2, u=SLOTS),
+            )
+
+        def quantize_y(h):
+            nc.vector.quantize_mx(out=y_codes[h][:].bitcast(FP8X4), scales=y_scales[:, HALF * h : HALF * (h + 1)], in_=y_grouped[:])
+            nc.sync.dma_start(
+                out=out_1[0, :, HALF * h : HALF * (h + 1), :].rearrange("p m t -> p (m t)").bitcast(I32),
+                in_=y_codes[h][:].bitcast(I32),
+            )
+
+        def turn_one(c, u, bank):
+            nc.tensor.transpose(
+                bank[:, P * u : P * (u + 1)],
+                y_t[:, HALF * u + P * c : HALF * u + P * (c + 1)], ident[:],
+            )
+
+        def turn(c, bank):
+            for u in range(SLOTS):
+                turn_one(c, u, bank)
+
+        def store_rows(h, c, bank, engine):
+            rows = y_rows[c % OUT_RING]
+            dealt = rows[:].rearrange("p (m u) -> p m u", u=SLOTS)
+            turned = bank[:].rearrange("p (u m) -> p m u", u=SLOTS)
+            if engine == "scalar":
+                nc.scalar.copy(out=dealt, in_=turned)
+            else:
+                nc.vector.tensor_copy(out=dealt, in_=turned)
+            nc.sync.dma_start(out=out_0[HALF * h + P * c : HALF * h + P * (c + 1), :], in_=rows[:])
+
+        nc.vector.memset(f_scales_first[:].bitcast(I32), 0)
+        nc.vector.memset(e_scales[:].bitcast(I32), 0)
+        nc.vector.memset(warm[:], 0.0)
+        nc.vector.memset(f_scales_rest[:].bitcast(I32), 0)
+        nc.scalar.activation(out=warm_out[:], in_=warm[:], func=ACT.Sigmoid)
+        load_e(0)
+        load_f(0)
+        for quadrant in range(4):
+            load_scale_rows(nc.sync, f_scales_first, pixel_scales[0, :, :FIRST], quadrant)
+        for quadrant in range(2):
+            load_scale_rows(nc.sync, e_scales, query_scales[0], quadrant)
+        for quadrant in range(2, 4):
+            load_scale_rows(nc.gpsimd, e_scales, query_scales[0], quadrant)
+        nc.sync.dma_start(out=w_raw[:], in_=pixel_weight.rearrange("(g k) -> g k", g=PASSES))
+        load_f(1)
+        for quadrant in range(4):
+            load_scale_rows(nc.sync, f_scales_rest, pixel_scales[0, :, FIRST:], quadrant)
+        load_t(0)
+        load_t(1)
+        load_f(2)
+        load_t(2)
+        load_e(1)
+        nc.sync.dma_start(out=consts_raw[:, 0, :SLOTS], in_=target_area.rearrange("(p u) -> p u", u=SLOTS))
+        nc.sync.dma_start(out=consts_raw[:, 1, :SLOTS], in_=target_gain.rearrange("(p u) -> p u", u=SLOTS))
+        for g in range(3, PASSES):
+            load_t(g)
+        make_identity(nc, ident[:])
+        nc.vector.memset(w_rows[:], 0.0)
+        nc.vector.memset(frame_scales4[:], 0)
+
+        deal_f(0)
+        nc.vector.tensor_copy(
+            out=w_rows[:PASSES].rearrange("g t (a e) -> g t a e", e=4),
+            in_=w_raw[:].rearrange("g (a t e) -> g t a e", t=SLOTS, e=4),
+        )
+
+        def bank_of(s, t):
+            return logit_bank[(SLOTS * s + t) % 3]
+
+        for t in range(SLOTS):
+            logits(0, t, bank_of(0, t))
+        for t in range(SLOTS):
+            nc.tensor.transpose(w_bank[:].rearrange("p (g t) -> p t g", t=SLOTS)[:, t, :], w_rows[:, t, :], ident[:])
+        for g in range(T_RING):
+            group_t_pool(g)
+        deal_f(1)
+        for s in range(1, LEAD):
+            for t in range(SLOTS):
+                logits(s, t, bank_of(s, t))
+
+        MID = PASSES + 1
+        spare = w_bank
+        done = [0]
+        areas = [PASSES]
+
+        for i in range(STEPS):
+            ahead = i + LEAD if i < MID else i + 1
+            back = i - LAG if i < MID else i - 2
+            if i == MID:
+                load_root_table()
+                predicted_area(PASSES - 1, spare)
+                for s in range(done[0], PASSES):
+                    for u in range(SLOTS):
+                        intersect(s, u)
+                done[0] = PASSES
+                inverses(spare)
+            else:
+                if i == MID + 1:
+                    logits(ahead, 0, bank_of(ahead, 0))
+                    logits(ahead, 1, bank_of(ahead, 1))
+                    for u in range(SLOTS):
+                        ratio(u)
+                        intersect(PASSES, u)
+                    done[0] = PASSES + 1
+                    logits(ahead, 2, bank_of(ahead, 2))
+                    logits(ahead, 3, bank_of(ahead, 3))
+                else:
+                    for t in range(SLOTS):
+                        if ahead < STEPS:
+                            logits(ahead, t, bank_of(ahead, t))
+                        if back == done[0]:
+                            intersect(back, t)
+                    if back == done[0]:
+                        done[0] = back + 1
+            if i < PASSES:
+                group_t_scalar(i)
+            if i == PASSES:
+                for s in range(PASSES - 1):
+                    predicted_area(s, spare)
+            if MID + 1 <= i < MID + 1 + SLOTS:
+                turn(i - MID - 1, spare)
+                store_rows(0, i - MID - 1, spare, "scalar")
+            if i >= MID + 1 + SLOTS:
+                for s in range(areas[0], i - 1):
+                    predicted_area(s, spare)
+                areas[0] = i - 1
+            if ahead == STEPS:
+                load_root_table()
+            if i == STEPS - 1:
+                quantize_h(i - 1)
+            weigh(i)
+            if i == 0:
+                nc.vector.tensor_copy(out=w_cols[:], in_=w_bank[:, : PASSES * SLOTS])
+            if i == 1:
+                deal_f(2)
+            if i == 2:
+                nc.vector.tensor_copy(out=consts[:], in_=consts_raw[:, :, :SLOTS])
+            if 1 <= i < STEPS - 1:
+                quantize_h(i - 1)
+            if i == 3:
+                group_frame()
+            if i == 4:
+                quantize_frame()
+            if i == 5:
+                spread_frame()
+            if 1 <= i <= PASSES:
+                quantize_t(i - 1)
+                if i - 1 + T_RING < PASSES:
+                    group_t_pool(i - 1 + T_RING)
+            if i == MID + 1:
+                group_y()
+            if i == MID + 2:
+                quantize_y(0)
+
+        predicted_area(STEPS - 2, spare)
+        for u in range(SLOTS):
+            intersect(STEPS - 2, u)
+        quantize_h(STEPS - 1)
+        predicted_area(STEPS - 1, spare)
+        for u in range(SLOTS):
+            intersect(STEPS - 1, u)
+        for u in range(SLOTS):
+            inverse_root(u, spare)
+        square_vector(0)
+        square_vector(1)
+        square(2)
+        square(3)
+        for u in range(SLOTS):
+            ratio(u)
+        group_y()
+        tail_banks = [logit_bank[0], logit_bank[1], logit_bank[2], spare]
+        for u in range(SLOTS):
+            for c in range(SLOTS):
+                turn_one(c, u, tail_banks[c])
+        for c in range(SLOTS - 1):
+            store_rows(1, c, tail_banks[c], "scalar")
+        quantize_y(1)
+        for quadrant in range(4):
+            nc.sync.dma_start(
+                out=out_2[0, 4 * quadrant : 4 * quadrant + 4, :].bitcast(I32),
+                in_=y_scales[32 * quadrant : 32 * quadrant + 4, :].bitcast(I32),
+            )
+        store_rows(1, SLOTS - 1, tail_banks[SLOTS - 1], "scalar")

@@ -30,7 +30,11 @@ LEAD = 2
 LAG = 3
 H_RING = 2
 T_RING = 2
-POOL_SLOTS = 3
+T_SCALAR = 40
+T_HEAD = 1
+B_FIRST = 0
+B_LAST = 4
+B_PREV = 0
 OUT_RING = 4
 
 
@@ -75,13 +79,14 @@ def tile_mask_dice_matching_k5_kernel(
         frame_codes = one("frame_codes", [P, PASSES, P], I32)
         frame_scales = one("frame_scales", [P, PASSES * P], U8)
         sig = tiles("sig", SIG_RING, [P, SLOTS * HALF], F32)
+        h_rows = tiles("h_rows", H_RING, [P, SLOTS * HALF], BF16)
         h_grouped = tiles("h_grouped", H_RING, [P, HALF * SLOTS], BF16)
         h_codes = tiles("h_codes", STEPS, [P, HALF], U32)
         h_scales = tiles("h_scales", STEPS, [P, HALF], U8)
         rsq = tiles("rsq", SLOTS, [P, HALF], F32)
         inv = tiles("inv", SLOTS, [P, HALF], F32)
-        y_t = one("y_t", [P, SLOTS * HALF], F32)
-        y_grouped = one("y_grouped", [P, HALF * SLOTS], BF16)
+        y_t = one("y_t", [P, SLOTS, HALF], F32)
+        y_grouped = one("y_grouped", [P, HALF, SLOTS], BF16)
         y_codes = tiles("y_codes", HALVES, [P, HALF], U32)
         y_scales = one("y_scales", [P, QUERIES], U8)
         y_rows = tiles("y_rows", OUT_RING, [P, TARGETS], F32)
@@ -121,8 +126,8 @@ def tile_mask_dice_matching_k5_kernel(
                 in_=f_raw[n][:].rearrange("p (g a t w) -> p g t a w", t=SLOTS, a=32, w=2),
             )
             nc.vector.tensor_copy(
-                out=f_scales[n][:].bitcast(I32).rearrange("p (g t a) -> p g t a", t=SLOTS, a=32),
-                in_=raw_scales.bitcast(I32).rearrange("p (g a t) -> p g t a", t=SLOTS, a=32),
+                out=f_scales[n][:].bitcast(I32).rearrange("p (g t a i) -> p g a t i", t=SLOTS, a=8, i=4),
+                in_=raw_scales.bitcast(I32).rearrange("p (g a i t) -> p g a t i", t=SLOTS, a=8, i=4),
             )
 
         def logits(s, t, bank):
@@ -139,32 +144,32 @@ def tile_mask_dice_matching_k5_kernel(
             )
             nc.scalar.activation(out=sig[s % SIG_RING][:, HALF * t : HALF * (t + 1)], in_=bank[:], func=ACT.Sigmoid)
 
-        def weigh(s):
-            g = s % PASSES
-            weights = w_bank if s < PASSES else w_cols
-            nc.vector.tensor_tensor(
-                out=h_grouped[s % H_RING][:].rearrange("p (c i t) -> p c t i", i=2, t=SLOTS),
-                in0=sig[s % SIG_RING][:].rearrange("p (t c i) -> p c t i", i=2, t=SLOTS),
-                in1=weights[:, SLOTS * g : SLOTS * (g + 1)].unsqueeze(1).unsqueeze(3).to_broadcast([P, HALF // 2, SLOTS, 2]),
-                op=ALU.mult,
+        def weigh(s, t, engine):
+            col = SLOTS * (s % PASSES) + t
+            dst = h_rows[s % H_RING][:, HALF * t : HALF * (t + 1)]
+            src = sig[s % SIG_RING][:, HALF * t : HALF * (t + 1)]
+            if engine == "scalar":
+                nc.scalar.activation(out=dst, in_=src, func=ACT.Copy, scale=w_cols[:, col : col + 1])
+            else:
+                nc.vector.tensor_scalar(out=dst, in0=src, scalar1=w_cols[:, col : col + 1], scalar2=None, op0=ALU.mult)
+
+        def group_h(s):
+            nc.vector.tensor_copy(
+                out=h_grouped[s % H_RING][:].rearrange("p (c i t) -> p c t i", i=4, t=SLOTS),
+                in_=h_rows[s % H_RING][:].rearrange("p (t c i) -> p c t i", i=4, t=SLOTS),
             )
 
         def quantize_h(s):
             nc.vector.quantize_mx(out=h_codes[s][:].bitcast(FP8X4), scales=h_scales[s][:], in_=h_grouped[s % H_RING][:])
 
-        def group_t_pool(g):
-            nc.gpsimd.tensor_scalar(
-                out=t_grouped[g % T_RING][:, : POOL_SLOTS * TARGETS].rearrange("p (u m j) -> p u m j", u=POOL_SLOTS, j=SLOTS),
-                in0=t_raw[:, g, :, :].rearrange("p j (m u) -> p u m j", u=SLOTS)[:, :POOL_SLOTS],
-                scalar1=1.0, scalar2=0.0, op0=ALU.mult, op1=ALU.add,
-            )
-
-        def group_t_scalar(g):
-            for u in range(POOL_SLOTS, SLOTS):
-                nc.scalar.copy(
-                    out=t_grouped[g % T_RING][:, u * TARGETS : (u + 1) * TARGETS].rearrange("p (m i j) -> p m j i", i=2, j=SLOTS),
-                    in_=t_raw[:, g, :, :].rearrange("p j (m i u) -> p u m j i", u=SLOTS, i=2)[:, u],
-                )
+        def group_t(g, engine):
+            dst = t_grouped[g % T_RING][:].rearrange("p (u k i j) -> p k u i j", u=SLOTS, i=2, j=SLOTS)
+            src = t_raw[:, g, :, :].rearrange("p j (k i u) -> p k u i j", u=SLOTS, i=2)
+            share = T_SCALAR if g >= T_HEAD else 0
+            if engine == "vector":
+                nc.vector.tensor_copy(out=dst[:, share:], in_=src[:, share:])
+            elif share:
+                nc.scalar.copy(out=dst[:, :share], in_=src[:, :share])
 
         def quantize_t(g):
             nc.vector.quantize_mx(out=t_codes[g][:].bitcast(FP8X4), scales=t_scales[g][:], in_=t_grouped[g % T_RING][:])
@@ -209,48 +214,43 @@ def tile_mask_dice_matching_k5_kernel(
                 start=(g == 0), stop=(g == PASSES - 1),
             )
 
-        def inverse_root(u, bank):
-            nc.scalar.activation(out=rsq[u][:], in_=bank[:], func=ACT.Abs_reciprocal_sqrt, bias=consts[:, 0, u : u + 1])
+        def inverse_root(u, bank, cols):
+            nc.scalar.activation(out=rsq[u][:, cols], in_=bank[:, cols], func=ACT.Abs_reciprocal_sqrt, bias=consts[:, 0, u : u + 1])
 
-        def square(u):
-            nc.scalar.activation(out=inv[u][:], in_=rsq[u][:], func=ACT.Square)
-
-        def square_vector(u):
-            nc.vector.tensor_tensor(out=inv[u][:], in0=rsq[u][:], in1=rsq[u][:], op=ALU.mult)
-
-        def inverses(bank):
-            for u in range(SLOTS + 1):
-                if u < SLOTS:
-                    inverse_root(u, bank)
-                if u >= 1:
-                    square(u - 1)
+        def square(u, cols, engine):
+            if engine == "scalar":
+                nc.scalar.activation(out=inv[u][:, cols], in_=rsq[u][:, cols], func=ACT.Square)
+            else:
+                nc.vector.tensor_tensor(out=inv[u][:, cols], in0=rsq[u][:, cols], in1=rsq[u][:, cols], op=ALU.mult)
 
         def load_root_table():
             nc.scalar.activation(out=warm_out[:], in_=ident[:, :8], func=ACT.Abs_reciprocal_sqrt, bias=1.0)
 
-        def ratio(u):
+        def ratio(u, cols):
             nc.vector.scalar_tensor_tensor(
-                out=y_t[:, HALF * u : HALF * (u + 1)], in0=acc[u][:], scalar=consts[:, 1, u : u + 1],
-                in1=inv[u][:], op0=ALU.mult, op1=ALU.mult,
+                out=y_t[:, u, cols], in0=acc[u][:, cols], scalar=consts[:, 1, u : u + 1],
+                in1=inv[u][:, cols], op0=ALU.mult, op1=ALU.mult,
             )
 
-        def group_y():
+        def group_y(cols):
             nc.vector.tensor_copy(
-                out=y_grouped[:].rearrange("p (c i u) -> p c u i", i=2, u=SLOTS),
-                in_=y_t[:].rearrange("p (u c i) -> p c u i", i=2, u=SLOTS),
+                out=y_grouped[:, cols, :].rearrange("p (c i) u -> p c u i", i=4),
+                in_=y_t[:, :, cols].rearrange("p u (c i) -> p c u i", i=4),
             )
 
-        def quantize_y(h):
-            nc.vector.quantize_mx(out=y_codes[h][:].bitcast(FP8X4), scales=y_scales[:, HALF * h : HALF * (h + 1)], in_=y_grouped[:])
+        def quantize_y(h, cols):
+            out_cols = slice(HALF * h + cols.start, HALF * h + cols.stop)
+            nc.vector.quantize_mx(out=y_codes[h][:, cols].bitcast(FP8X4), scales=y_scales[:, out_cols],
+                                  in_=y_grouped[:, cols, :].rearrange("p c u -> p (c u)"))
             nc.sync.dma_start(
-                out=out_1[0, :, HALF * h : HALF * (h + 1), :].rearrange("p m t -> p (m t)").bitcast(I32),
-                in_=y_codes[h][:].bitcast(I32),
+                out=out_1[0, :, out_cols, :].rearrange("p m t -> p (m t)").bitcast(I32),
+                in_=y_codes[h][:, cols].bitcast(I32),
             )
 
         def turn_one(c, u, bank):
             nc.tensor.transpose(
                 bank[:, P * u : P * (u + 1)],
-                y_t[:, HALF * u + P * c : HALF * u + P * (c + 1)], ident[:],
+                y_t[:, u, P * c : P * (c + 1)], ident[:],
             )
 
         def turn(c, bank):
@@ -278,9 +278,9 @@ def tile_mask_dice_matching_k5_kernel(
             load_scale_rows(nc.sync, f_scales_first, pixel_scales[0, :, :FIRST], quadrant)
         for quadrant in range(2):
             load_scale_rows(nc.sync, e_scales, query_scales[0], quadrant)
+        nc.gpsimd.dma_start(out=w_raw[:], in_=pixel_weight.rearrange("(g k) -> g k", g=PASSES))
         for quadrant in range(2, 4):
             load_scale_rows(nc.gpsimd, e_scales, query_scales[0], quadrant)
-        nc.sync.dma_start(out=w_raw[:], in_=pixel_weight.rearrange("(g k) -> g k", g=PASSES))
         load_f(1)
         for quadrant in range(4):
             load_scale_rows(nc.sync, f_scales_rest, pixel_scales[0, :, FIRST:], quadrant)
@@ -297,126 +297,148 @@ def tile_mask_dice_matching_k5_kernel(
         nc.vector.memset(w_rows[:], 0.0)
         nc.vector.memset(frame_scales4[:], 0)
 
-        deal_f(0)
         nc.vector.tensor_copy(
             out=w_rows[:PASSES].rearrange("g t (a e) -> g t a e", e=4),
             in_=w_raw[:].rearrange("g (a t e) -> g t a e", t=SLOTS, e=4),
         )
+        deal_f(0)
 
         def bank_of(s, t):
             return logit_bank[(SLOTS * s + t) % 3]
 
         for t in range(SLOTS):
-            logits(0, t, bank_of(0, t))
+            nc.tensor.transpose(w_bank[:, P * t : P * (t + 1)], w_rows[:, t, :], ident[:])
+        nc.vector.tensor_copy(
+            out=w_cols[:].rearrange("p (g t) -> p g t", t=SLOTS),
+            in_=w_bank[:].rearrange("p (t g) -> p g t", t=SLOTS)[:, :PASSES, :],
+        )
         for t in range(SLOTS):
-            nc.tensor.transpose(w_bank[:].rearrange("p (g t) -> p t g", t=SLOTS)[:, t, :], w_rows[:, t, :], ident[:])
-        for g in range(T_RING):
-            group_t_pool(g)
-        deal_f(1)
+            logits(0, t, bank_of(0, t))
         for s in range(1, LEAD):
             for t in range(SLOTS):
                 logits(s, t, bank_of(s, t))
 
         MID = PASSES + 1
         spare = w_bank
+        whole = slice(0, HALF)
         done = [0]
-        areas = [PASSES]
+        areas = [0]
+
+        def scalar_slots(s):
+            return B_FIRST if 2 <= s < PASSES else {STEPS - 1: B_LAST, STEPS - 2: B_PREV}.get(s, 0)
+
+        def areas_upto(s):
+            while areas[0] <= s:
+                predicted_area(areas[0], spare)
+                areas[0] = areas[0] + 1
 
         for i in range(STEPS):
-            ahead = i + LEAD if i < MID else i + 1
+            ahead = i + LEAD
             back = i - LAG if i < MID else i - 2
+            if i == 0:
+                deal_f(1)
             if i == MID:
                 load_root_table()
-                predicted_area(PASSES - 1, spare)
+                areas_upto(PASSES - 1)
                 for s in range(done[0], PASSES):
                     for u in range(SLOTS):
                         intersect(s, u)
                 done[0] = PASSES
-                inverses(spare)
+                for u in range(SLOTS + 1):
+                    if u < SLOTS:
+                        inverse_root(u, spare, whole)
+                    if u >= 1:
+                        square(u - 1, whole, "scalar")
             else:
                 if i == MID + 1:
-                    logits(ahead, 0, bank_of(ahead, 0))
-                    logits(ahead, 1, bank_of(ahead, 1))
-                    for u in range(SLOTS):
-                        ratio(u)
-                        intersect(PASSES, u)
-                    done[0] = PASSES + 1
-                    logits(ahead, 2, bank_of(ahead, 2))
-                    logits(ahead, 3, bank_of(ahead, 3))
-                else:
                     for t in range(SLOTS):
-                        if ahead < STEPS:
-                            logits(ahead, t, bank_of(ahead, t))
-                        if back == done[0]:
-                            intersect(back, t)
-                    if back == done[0]:
-                        done[0] = back + 1
+                        logits(ahead - 1, t, bank_of(ahead - 1, t))
+                for t in range(SLOTS):
+                    if ahead < STEPS:
+                        logits(ahead, t, bank_of(ahead, t))
+                    if back == done[0] and i != MID + 1:
+                        intersect(back, t)
+                if back == done[0] and i != MID + 1:
+                    done[0] = back + 1
+            nxt = i + 1
+            if nxt < STEPS:
+                for t in range(scalar_slots(nxt)):
+                    weigh(nxt, t, "scalar")
             if i < PASSES:
-                group_t_scalar(i)
-            if i == PASSES:
-                for s in range(PASSES - 1):
-                    predicted_area(s, spare)
-            if MID + 1 <= i < MID + 1 + SLOTS:
-                turn(i - MID - 1, spare)
-                store_rows(0, i - MID - 1, spare, "scalar")
-            if i >= MID + 1 + SLOTS:
-                for s in range(areas[0], i - 1):
-                    predicted_area(s, spare)
-                areas[0] = i - 1
-            if ahead == STEPS:
-                load_root_table()
+                group_t(i, "scalar")
+            if 6 <= i <= PASSES:
+                areas_upto(min(3 * (i - 6) - 1, i - 2))
+            if MID + 2 <= i < MID + 4:
+                for c in range(2 * (i - MID - 2), 2 * (i - MID - 1)):
+                    turn(c, spare)
+                    store_rows(0, c, spare, "scalar")
+            if i >= MID + 4:
+                areas_upto(i - 2)
             if i == STEPS - 1:
+                load_root_table()
+            for t in range(scalar_slots(i), SLOTS):
+                weigh(i, t, "vector")
+            if i >= 1:
                 quantize_h(i - 1)
-            weigh(i)
-            if i == 0:
-                nc.vector.tensor_copy(out=w_cols[:], in_=w_bank[:, : PASSES * SLOTS])
+            group_h(i)
+            if 1 <= i <= PASSES:
+                quantize_t(i - 1)
+            if i < PASSES:
+                group_t(i, "vector")
             if i == 1:
                 deal_f(2)
             if i == 2:
                 nc.vector.tensor_copy(out=consts[:], in_=consts_raw[:, :, :SLOTS])
-            if 1 <= i < STEPS - 1:
-                quantize_h(i - 1)
             if i == 3:
                 group_frame()
             if i == 4:
                 quantize_frame()
             if i == 5:
                 spread_frame()
-            if 1 <= i <= PASSES:
-                quantize_t(i - 1)
-                if i - 1 + T_RING < PASSES:
-                    group_t_pool(i - 1 + T_RING)
             if i == MID + 1:
-                group_y()
+                for u in range(SLOTS):
+                    ratio(u, whole)
+                    intersect(PASSES, u)
+                done[0] = PASSES + 1
+                group_y(whole)
             if i == MID + 2:
-                quantize_y(0)
+                quantize_y(0, whole)
 
-        predicted_area(STEPS - 2, spare)
+        areas_upto(STEPS - 2)
         for u in range(SLOTS):
             intersect(STEPS - 2, u)
         quantize_h(STEPS - 1)
-        predicted_area(STEPS - 1, spare)
+        areas_upto(STEPS - 1)
         for u in range(SLOTS):
             intersect(STEPS - 1, u)
+        first, second = slice(0, HALF // 2), slice(HALF // 2, HALF)
+        tail_banks = [logit_bank[0], logit_bank[1], logit_bank[2], logit_bank[0]]
         for u in range(SLOTS):
-            inverse_root(u, spare)
-        square_vector(0)
-        square_vector(1)
-        square(2)
-        square(3)
+            inverse_root(u, spare, first)
         for u in range(SLOTS):
-            ratio(u)
-        group_y()
-        tail_banks = [logit_bank[0], logit_bank[1], logit_bank[2], spare]
+            inverse_root(u, spare, second)
         for u in range(SLOTS):
-            for c in range(SLOTS):
-                turn_one(c, u, tail_banks[c])
-        for c in range(SLOTS - 1):
-            store_rows(1, c, tail_banks[c], "scalar")
-        quantize_y(1)
+            square(u, first, "vector")
+        for u in range(SLOTS):
+            ratio(u, first)
+        for u in range(SLOTS):
+            square(u, second, "scalar")
+        turn(0, tail_banks[0])
+        turn(1, tail_banks[1])
+        store_rows(1, 0, tail_banks[0], "scalar")
+        store_rows(1, 1, tail_banks[1], "scalar")
+        for u in range(SLOTS):
+            ratio(u, second)
+        turn(2, tail_banks[2])
+        turn(3, tail_banks[3])
+        group_y(first)
+        group_y(second)
+        quantize_y(1, first)
+        store_rows(1, 2, tail_banks[2], "scalar")
+        quantize_y(1, second)
+        store_rows(1, 3, tail_banks[3], "scalar")
         for quadrant in range(4):
             nc.sync.dma_start(
                 out=out_2[0, 4 * quadrant : 4 * quadrant + 4, :].bitcast(I32),
                 in_=y_scales[32 * quadrant : 32 * quadrant + 4, :].bitcast(I32),
             )
-        store_rows(1, SLOTS - 1, tail_banks[SLOTS - 1], "scalar")

@@ -28,13 +28,10 @@ FIRST = F_CHUNKS[0][1] * K_PASS
 SIG_RING = 4
 LEAD = 2
 LAG = 3
-H_RING = 2
+H_RING = 3
 T_RING = 2
-T_SCALAR = 40
+T_SCALAR = 36
 T_HEAD = 1
-B_FIRST = 0
-B_LAST = 4
-B_PREV = 0
 OUT_RING = 4
 
 
@@ -79,7 +76,6 @@ def tile_mask_dice_matching_k5_kernel(
         frame_codes = one("frame_codes", [P, PASSES, P], I32)
         frame_scales = one("frame_scales", [P, PASSES * P], U8)
         sig = tiles("sig", SIG_RING, [P, SLOTS * HALF], F32)
-        h_rows = tiles("h_rows", H_RING, [P, SLOTS * HALF], BF16)
         h_grouped = tiles("h_grouped", H_RING, [P, HALF * SLOTS], BF16)
         h_codes = tiles("h_codes", STEPS, [P, HALF], U32)
         h_scales = tiles("h_scales", STEPS, [P, HALF], U8)
@@ -144,19 +140,13 @@ def tile_mask_dice_matching_k5_kernel(
             )
             nc.scalar.activation(out=sig[s % SIG_RING][:, HALF * t : HALF * (t + 1)], in_=bank[:], func=ACT.Sigmoid)
 
-        def weigh(s, t, engine):
-            col = SLOTS * (s % PASSES) + t
-            dst = h_rows[s % H_RING][:, HALF * t : HALF * (t + 1)]
-            src = sig[s % SIG_RING][:, HALF * t : HALF * (t + 1)]
-            if engine == "scalar":
-                nc.scalar.activation(out=dst, in_=src, func=ACT.Copy, scale=w_cols[:, col : col + 1])
-            else:
-                nc.vector.tensor_scalar(out=dst, in0=src, scalar1=w_cols[:, col : col + 1], scalar2=None, op0=ALU.mult)
-
-        def group_h(s):
-            nc.vector.tensor_copy(
-                out=h_grouped[s % H_RING][:].rearrange("p (c i t) -> p c t i", i=4, t=SLOTS),
-                in_=h_rows[s % H_RING][:].rearrange("p (t c i) -> p c t i", i=4, t=SLOTS),
+        def weigh(s):
+            g = s % PASSES
+            nc.vector.tensor_tensor(
+                out=h_grouped[s % H_RING][:].rearrange("p (c i t) -> p c t i", i=2, t=SLOTS),
+                in0=sig[s % SIG_RING][:].rearrange("p (t c i) -> p c t i", i=2, t=SLOTS),
+                in1=w_cols[:, SLOTS * g : SLOTS * (g + 1)].unsqueeze(1).unsqueeze(3).to_broadcast([P, HALF // 2, SLOTS, 2]),
+                op=ALU.mult,
             )
 
         def quantize_h(s):
@@ -232,19 +222,24 @@ def tile_mask_dice_matching_k5_kernel(
                 in1=inv[u][:, cols], op0=ALU.mult, op1=ALU.mult,
             )
 
-        def group_y(cols):
-            nc.vector.tensor_copy(
-                out=y_grouped[:, cols, :].rearrange("p (c i) u -> p c u i", i=4),
-                in_=y_t[:, :, cols].rearrange("p u (c i) -> p c u i", i=4),
-            )
+        def group_y(cols, engine):
+            if engine == "scalar":
+                nc.scalar.copy(out=y_grouped[:, cols, :], in_=y_t[:, :, cols].rearrange("p u c -> p c u"))
+            else:
+                nc.vector.tensor_copy(
+                    out=y_grouped[:, cols, :].rearrange("p (c i) u -> p c u i", i=2),
+                    in_=y_t[:, :, cols].rearrange("p u (c i) -> p c u i", i=2),
+                )
 
         def quantize_y(h, cols):
             out_cols = slice(HALF * h + cols.start, HALF * h + cols.stop)
             nc.vector.quantize_mx(out=y_codes[h][:, cols].bitcast(FP8X4), scales=y_scales[:, out_cols],
                                   in_=y_grouped[:, cols, :].rearrange("p c u -> p (c u)"))
+
+        def store_codes(h):
             nc.sync.dma_start(
-                out=out_1[0, :, out_cols, :].rearrange("p m t -> p (m t)").bitcast(I32),
-                in_=y_codes[h][:, cols].bitcast(I32),
+                out=out_1[0, :, HALF * h : HALF * (h + 1), :].rearrange("p m t -> p (m t)").bitcast(I32),
+                in_=y_codes[h][:].bitcast(I32),
             )
 
         def turn_one(c, u, bank):
@@ -278,9 +273,9 @@ def tile_mask_dice_matching_k5_kernel(
             load_scale_rows(nc.sync, f_scales_first, pixel_scales[0, :, :FIRST], quadrant)
         for quadrant in range(2):
             load_scale_rows(nc.sync, e_scales, query_scales[0], quadrant)
-        nc.gpsimd.dma_start(out=w_raw[:], in_=pixel_weight.rearrange("(g k) -> g k", g=PASSES))
         for quadrant in range(2, 4):
             load_scale_rows(nc.gpsimd, e_scales, query_scales[0], quadrant)
+        nc.gpsimd.dma_start(out=w_raw[:], in_=pixel_weight.rearrange("(g k) -> g k", g=PASSES))
         load_f(1)
         for quadrant in range(4):
             load_scale_rows(nc.sync, f_scales_rest, pixel_scales[0, :, FIRST:], quadrant)
@@ -297,23 +292,23 @@ def tile_mask_dice_matching_k5_kernel(
         nc.vector.memset(w_rows[:], 0.0)
         nc.vector.memset(frame_scales4[:], 0)
 
+        deal_f(0)
         nc.vector.tensor_copy(
             out=w_rows[:PASSES].rearrange("g t (a e) -> g t a e", e=4),
             in_=w_raw[:].rearrange("g (a t e) -> g t a e", t=SLOTS, e=4),
         )
-        deal_f(0)
 
         def bank_of(s, t):
             return logit_bank[(SLOTS * s + t) % 3]
 
+        for t in range(SLOTS):
+            logits(0, t, bank_of(0, t))
         for t in range(SLOTS):
             nc.tensor.transpose(w_bank[:, P * t : P * (t + 1)], w_rows[:, t, :], ident[:])
         nc.vector.tensor_copy(
             out=w_cols[:].rearrange("p (g t) -> p g t", t=SLOTS),
             in_=w_bank[:].rearrange("p (t g) -> p g t", t=SLOTS)[:, :PASSES, :],
         )
-        for t in range(SLOTS):
-            logits(0, t, bank_of(0, t))
         for s in range(1, LEAD):
             for t in range(SLOTS):
                 logits(s, t, bank_of(s, t))
@@ -321,69 +316,74 @@ def tile_mask_dice_matching_k5_kernel(
         MID = PASSES + 1
         spare = w_bank
         whole = slice(0, HALF)
-        done = [0]
+        first, second = slice(0, HALF // 2), slice(HALF // 2, HALF)
         areas = [0]
-
-        def scalar_slots(s):
-            return B_FIRST if 2 <= s < PASSES else {STEPS - 1: B_LAST, STEPS - 2: B_PREV}.get(s, 0)
+        last_area_bank = bank_of(STEPS - 1, 1)
 
         def areas_upto(s):
             while areas[0] <= s:
-                predicted_area(areas[0], spare)
+                predicted_area(areas[0], spare if areas[0] < PASSES else last_area_bank)
                 areas[0] = areas[0] + 1
+
+        def intersect_step(s):
+            for u in range(SLOTS):
+                intersect(s, u)
+
+        def logits_step(s, back):
+            for t in range(SLOTS):
+                logits(s, t, bank_of(s, t))
+                if back is not None:
+                    intersect(back, t)
 
         for i in range(STEPS):
             ahead = i + LEAD
-            back = i - LAG if i < MID else i - 2
             if i == 0:
                 deal_f(1)
+            if i < MID:
+                logits_step(ahead, i - LAG if i >= LAG else None)
+            if i == MID - 1:
+                logits_step(ahead + 1, i + 1 - LAG)
+            if i < PASSES:
+                group_t(i, "scalar")
+            if 6 < i < MID:
+                areas_upto(min(4 * (i - 6) - 1, i - 2))
             if i == MID:
                 load_root_table()
                 areas_upto(PASSES - 1)
-                for s in range(done[0], PASSES):
-                    for u in range(SLOTS):
-                        intersect(s, u)
-                done[0] = PASSES
+                intersect_step(PASSES - 1)
                 for u in range(SLOTS + 1):
                     if u < SLOTS:
                         inverse_root(u, spare, whole)
                     if u >= 1:
                         square(u - 1, whole, "scalar")
-            else:
-                if i == MID + 1:
-                    for t in range(SLOTS):
-                        logits(ahead - 1, t, bank_of(ahead - 1, t))
-                for t in range(SLOTS):
-                    if ahead < STEPS:
-                        logits(ahead, t, bank_of(ahead, t))
-                    if back == done[0] and i != MID + 1:
-                        intersect(back, t)
-                if back == done[0] and i != MID + 1:
-                    done[0] = back + 1
-            nxt = i + 1
-            if nxt < STEPS:
-                for t in range(scalar_slots(nxt)):
-                    weigh(nxt, t, "scalar")
-            if i < PASSES:
-                group_t(i, "scalar")
-            if 6 <= i <= PASSES:
-                areas_upto(min(3 * (i - 6) - 1, i - 2))
-            if MID + 2 <= i < MID + 4:
-                for c in range(2 * (i - MID - 2), 2 * (i - MID - 1)):
-                    turn(c, spare)
-                    store_rows(0, c, spare, "scalar")
-            if i >= MID + 4:
+            if i == MID + 1:
+                for t in range(SLOTS - 1):
+                    logits(ahead, t, bank_of(ahead, t))
+            if MID + 1 < i and ahead < STEPS:
+                logits_step(ahead, i - 2)
+            if MID + 2 <= i < MID + 1 + SLOTS:
+                turn(i - MID - 1, spare)
+                store_rows(0, i - MID - 1, spare, "scalar")
+            if ahead == STEPS - 1:
+                group_y(whole, "scalar")
+            if ahead >= STEPS:
+                areas_upto(i - 3)
+                intersect_step(i - 2)
                 areas_upto(i - 2)
             if i == STEPS - 1:
                 load_root_table()
-            for t in range(scalar_slots(i), SLOTS):
-                weigh(i, t, "vector")
-            if i >= 1:
+            if i == STEPS - 1:
                 quantize_h(i - 1)
-            group_h(i)
+                areas_upto(i - 1)
+                intersect_step(i - 1)
+            weigh(i)
+            if i == 0:
+                group_t(0, "vector")
+            if 1 <= i < STEPS - 1:
+                quantize_h(i - 1)
             if 1 <= i <= PASSES:
                 quantize_t(i - 1)
-            if i < PASSES:
+            if 1 <= i < PASSES:
                 group_t(i, "vector")
             if i == 1:
                 deal_f(2)
@@ -399,24 +399,23 @@ def tile_mask_dice_matching_k5_kernel(
                 for u in range(SLOTS):
                     ratio(u, whole)
                     intersect(PASSES, u)
-                done[0] = PASSES + 1
-                group_y(whole)
-            if i == MID + 2:
+                    if u == 1:
+                        logits(ahead, SLOTS - 1, bank_of(ahead, SLOTS - 1))
+                turn(0, spare)
+                store_rows(0, 0, spare, "scalar")
+            if i == STEPS - 1:
                 quantize_y(0, whole)
+                store_codes(0)
 
-        areas_upto(STEPS - 2)
-        for u in range(SLOTS):
-            intersect(STEPS - 2, u)
         quantize_h(STEPS - 1)
         areas_upto(STEPS - 1)
+        intersect_step(STEPS - 1)
+        free = [bank for bank in logit_bank if bank is not last_area_bank]
+        tail_banks = free + [spare, free[0]]
         for u in range(SLOTS):
-            intersect(STEPS - 1, u)
-        first, second = slice(0, HALF // 2), slice(HALF // 2, HALF)
-        tail_banks = [logit_bank[0], logit_bank[1], logit_bank[2], logit_bank[0]]
+            inverse_root(u, last_area_bank, first)
         for u in range(SLOTS):
-            inverse_root(u, spare, first)
-        for u in range(SLOTS):
-            inverse_root(u, spare, second)
+            inverse_root(u, last_area_bank, second)
         for u in range(SLOTS):
             square(u, first, "vector")
         for u in range(SLOTS):
@@ -431,11 +430,12 @@ def tile_mask_dice_matching_k5_kernel(
             ratio(u, second)
         turn(2, tail_banks[2])
         turn(3, tail_banks[3])
-        group_y(first)
-        group_y(second)
+        group_y(first, "vector")
+        group_y(second, "vector")
         quantize_y(1, first)
         store_rows(1, 2, tail_banks[2], "scalar")
         quantize_y(1, second)
+        store_codes(1)
         store_rows(1, 3, tail_banks[3], "scalar")
         for quadrant in range(4):
             nc.sync.dma_start(

@@ -28,9 +28,9 @@ FIRST = F_CHUNKS[0][1] * K_PASS
 SIG_RING = 4
 LEAD = 2
 LAG = 3
-H_RING = 3
-T_RING = 2
-T_SCALAR = 36
+RING = 3
+T_POOL = 24
+T_SCALAR = 32
 T_HEAD = 1
 OUT_RING = 4
 
@@ -66,23 +66,20 @@ def tile_mask_dice_matching_k5_kernel(
         consts = one("consts", [P, 2, SLOTS], F32)
         warm = one("warm", [P, 8], F32)
         warm_out = one("warm_out", [P, 8], F32)
-        t_raw = one("t_raw", [P, PASSES, SLOTS, TARGETS], BF16)
-        t_grouped = tiles("t_grouped", T_RING, [P, SLOTS * TARGETS], BF16)
-        t_codes = tiles("t_codes", PASSES, [P, TARGETS], U32)
-        t_scales = tiles("t_scales", PASSES, [P, TARGETS], U8)
+        t_raw = tiles("t_raw", PASSES, [P, SLOTS, TARGETS], BF16)
         frame_grouped = one("frame_grouped", [P, PASSES, 4, SLOTS], BF16)
         frame_codes4 = one("frame_codes4", [P, PASSES * 4], I32)
         frame_scales4 = one("frame_scales4", [P, PASSES * 4], U8)
         frame_codes = one("frame_codes", [P, PASSES, P], I32)
         frame_scales = one("frame_scales", [P, PASSES * P], U8)
         sig = tiles("sig", SIG_RING, [P, SLOTS * HALF], F32)
-        h_grouped = tiles("h_grouped", H_RING, [P, HALF * SLOTS], BF16)
-        h_codes = tiles("h_codes", STEPS, [P, HALF], U32)
-        h_scales = tiles("h_scales", STEPS, [P, HALF], U8)
+        grouped = [g[:].rearrange("p (a c) -> p a c", a=2) for g in tiles("grouped", RING, [P, 2 * SLOTS * HALF], BF16)]
+        codes = [one("codes%d" % s, [P, 2 * HALF if s < PASSES else HALF], U32) for s in range(STEPS)]
+        scales = [one("scales%d" % s, [P, 2 * HALF if s < PASSES else HALF], U8) for s in range(STEPS)]
         rsq = tiles("rsq", SLOTS, [P, HALF], F32)
         inv = tiles("inv", SLOTS, [P, HALF], F32)
-        y_t = one("y_t", [P, SLOTS, HALF], F32)
-        y_grouped = one("y_grouped", [P, HALF, SLOTS], BF16)
+        y_t = one("y_t", [P, SLOTS * HALF], F32)[:].rearrange("p (u c) -> p u c", u=SLOTS)
+        y_grouped = one("y_grouped", [P, HALF * SLOTS], BF16)[:].rearrange("p (c u) -> p c u", u=SLOTS)
         y_codes = tiles("y_codes", HALVES, [P, HALF], U32)
         y_scales = one("y_scales", [P, QUERIES], U8)
         y_rows = tiles("y_rows", OUT_RING, [P, TARGETS], F32)
@@ -100,27 +97,29 @@ def tile_mask_dice_matching_k5_kernel(
                 in_=rows[4 * quadrant : 4 * quadrant + 4, :].bitcast(I32),
             )
 
-        def load_e(h):
-            nc.sync.dma_start(out=e_codes[h][:].bitcast(I32),
+        def load_e(h, queue):
+            queue.dma_start(out=e_codes[h][:].bitcast(I32),
                               in_=query_words[0, :, 2 * HALF * h : 2 * HALF * (h + 1)].bitcast(I32))
 
-        def load_f(n):
+        def load_f(n, queue):
             a, b = F_CHUNKS[n]
-            nc.sync.dma_start(out=f_raw[n][:], in_=pixel_words[0, :, 2 * K_PASS * a : 2 * K_PASS * b].bitcast(I32))
+            queue.dma_start(out=f_raw[n][:], in_=pixel_words[0, :, 2 * K_PASS * a : 2 * K_PASS * b].bitcast(I32))
 
         t_view = target_masks.rearrange("(g a t e) c -> g e a t c", g=PASSES, t=SLOTS, e=4)
 
         def load_t(g):
             for e in range(4):
-                nc.sync.dma_start(out=t_raw[e:P:4, g, :, :], in_=t_view[g, e])
+                nc.sync.dma_start(out=t_raw[g][e:P:4, :, :], in_=t_view[g, e])
 
-        def deal_f(n):
-            a, b = F_CHUNKS[n]
-            raw_scales = f_scales_first[:] if n == 0 else f_scales_rest[:, K_PASS * a - FIRST : K_PASS * b - FIRST]
+        def deal_f_codes(n):
             nc.vector.tensor_copy(
                 out=f_codes[n][:].bitcast(I32).rearrange("p (g t a w) -> p g t a w", t=SLOTS, a=32, w=2),
                 in_=f_raw[n][:].rearrange("p (g a t w) -> p g t a w", t=SLOTS, a=32, w=2),
             )
+
+        def deal_f_scales(n):
+            a, b = F_CHUNKS[n]
+            raw_scales = f_scales_first[:] if n == 0 else f_scales_rest[:, K_PASS * a - FIRST : K_PASS * b - FIRST]
             nc.vector.tensor_copy(
                 out=f_scales[n][:].bitcast(I32).rearrange("p (g t a i) -> p g a t i", t=SLOTS, a=8, i=4),
                 in_=raw_scales.bitcast(I32).rearrange("p (g a i t) -> p g a t i", t=SLOTS, a=8, i=4),
@@ -142,33 +141,41 @@ def tile_mask_dice_matching_k5_kernel(
 
         def weigh(s):
             g = s % PASSES
+            weights = w_bank if s < PASSES - 1 and T_POOL else w_cols
             nc.vector.tensor_tensor(
-                out=h_grouped[s % H_RING][:].rearrange("p (c i t) -> p c t i", i=2, t=SLOTS),
+                out=grouped[s % RING][:, 0, :].rearrange("p (c i t) -> p c t i", i=2, t=SLOTS),
                 in0=sig[s % SIG_RING][:].rearrange("p (t c i) -> p c t i", i=2, t=SLOTS),
-                in1=w_cols[:, SLOTS * g : SLOTS * (g + 1)].unsqueeze(1).unsqueeze(3).to_broadcast([P, HALF // 2, SLOTS, 2]),
+                in1=weights[:, SLOTS * g : SLOTS * (g + 1)].unsqueeze(1).unsqueeze(3).to_broadcast([P, HALF // 2, SLOTS, 2]),
                 op=ALU.mult,
             )
 
-        def quantize_h(s):
-            nc.vector.quantize_mx(out=h_codes[s][:].bitcast(FP8X4), scales=h_scales[s][:], in_=h_grouped[s % H_RING][:])
+        def quantize(s):
+            src = grouped[s % RING][:].rearrange("p a c -> p (a c)") if s < PASSES else grouped[s % RING][:, 0, :]
+            nc.vector.quantize_mx(out=codes[s][:].bitcast(FP8X4), scales=scales[s][:], in_=src)
 
         def group_t(g, engine):
-            dst = t_grouped[g % T_RING][:].rearrange("p (u k i j) -> p k u i j", u=SLOTS, i=2, j=SLOTS)
-            src = t_raw[:, g, :, :].rearrange("p j (k i u) -> p k u i j", u=SLOTS, i=2)
-            share = T_SCALAR if g >= T_HEAD else 0
+            dst = grouped[g % RING][:, 1, :].rearrange("p (u k i j) -> p k u j i", u=SLOTS, i=2, j=SLOTS)
+            src = t_raw[g][:].rearrange("p j (k i u) -> p k u j i", u=SLOTS, i=2)
+            share = T_POOL + T_SCALAR if g >= T_HEAD else 0
             if engine == "vector":
-                nc.vector.tensor_copy(out=dst[:, share:], in_=src[:, share:])
-            elif share:
-                nc.scalar.copy(out=dst[:, :share], in_=src[:, :share])
-
-        def quantize_t(g):
-            nc.vector.quantize_mx(out=t_codes[g][:].bitcast(FP8X4), scales=t_scales[g][:], in_=t_grouped[g % T_RING][:])
+                if share < 64:
+                    nc.vector.tensor_copy(out=dst[:, share:], in_=src[:, share:])
+            elif engine == "scalar":
+                if share:
+                    nc.scalar.copy(out=dst[:, T_POOL:share], in_=src[:, T_POOL:share])
+            elif T_POOL:
+                nc.gpsimd.tensor_scalar(
+                    out=grouped[g % RING][:, 1, :].rearrange("p (u m j) -> p u m j", u=SLOTS, j=SLOTS)[:, :, : 2 * T_POOL],
+                    in0=t_raw[g][:].rearrange("p j (m u) -> p u m j", u=SLOTS)[:, :, : 2 * T_POOL],
+                    scalar1=1.0, scalar2=0.0, op0=ALU.mult, op1=ALU.add,
+                )
 
         def group_frame():
-            nc.vector.tensor_copy(
-                out=frame_grouped[:],
-                in_=t_raw[:, :, :, TARGETS - 1].unsqueeze(2).to_broadcast([P, PASSES, 4, SLOTS]),
-            )
+            for g in range(PASSES):
+                nc.scalar.copy(
+                    out=frame_grouped[:, g],
+                    in_=t_raw[g][:, :, TARGETS - 1].unsqueeze(1).to_broadcast([P, 4, SLOTS]),
+                )
 
         def quantize_frame():
             nc.vector.quantize_mx(out=frame_codes4[:].bitcast(FP8X4), scales=frame_scales4[:],
@@ -188,9 +195,9 @@ def tile_mask_dice_matching_k5_kernel(
             g = s % PASSES
             nc.tensor.matmul_mx(
                 out=acc[u][:],
-                lhsT=t_codes[g][:, P * u : P * (u + 1)].bitcast(FP8X4),
-                lhsT_scale=t_scales[g][:, P * u : P * (u + 1)],
-                rhs=h_codes[s][:].bitcast(FP8X4), rhs_scale=h_scales[s][:],
+                lhsT=codes[g][:, HALF + P * u : HALF + P * (u + 1)].bitcast(FP8X4),
+                lhsT_scale=scales[g][:, HALF + P * u : HALF + P * (u + 1)],
+                rhs=codes[s][:, :HALF].bitcast(FP8X4), rhs_scale=scales[s][:, :HALF],
                 start=(g == 0), stop=(g == PASSES - 1),
             )
 
@@ -200,7 +207,7 @@ def tile_mask_dice_matching_k5_kernel(
                 out=bank[:],
                 lhsT=frame_codes[:, g, :].bitcast(FP8X4),
                 lhsT_scale=frame_scales[:, P * g : P * (g + 1)],
-                rhs=h_codes[s][:].bitcast(FP8X4), rhs_scale=h_scales[s][:],
+                rhs=codes[s][:, :HALF].bitcast(FP8X4), rhs_scale=scales[s][:, :HALF],
                 start=(g == 0), stop=(g == PASSES - 1),
             )
 
@@ -223,13 +230,12 @@ def tile_mask_dice_matching_k5_kernel(
             )
 
         def group_y(cols, engine):
+            dst = y_grouped[:, cols, :].rearrange("p (c i) u -> p c u i", i=2)
+            src = y_t[:, :, cols].rearrange("p u (c i) -> p c u i", i=2)
             if engine == "scalar":
-                nc.scalar.copy(out=y_grouped[:, cols, :], in_=y_t[:, :, cols].rearrange("p u c -> p c u"))
+                nc.scalar.copy(out=dst, in_=src)
             else:
-                nc.vector.tensor_copy(
-                    out=y_grouped[:, cols, :].rearrange("p (c i) u -> p c u i", i=2),
-                    in_=y_t[:, :, cols].rearrange("p u (c i) -> p c u i", i=2),
-                )
+                nc.vector.tensor_copy(out=dst, in_=src)
 
         def quantize_y(h, cols):
             out_cols = slice(HALF * h + cols.start, HALF * h + cols.stop)
@@ -252,7 +258,7 @@ def tile_mask_dice_matching_k5_kernel(
             for u in range(SLOTS):
                 turn_one(c, u, bank)
 
-        def store_rows(h, c, bank, engine):
+        def store_rows(h, c, bank, engine, queue=nc.sync):
             rows = y_rows[c % OUT_RING]
             dealt = rows[:].rearrange("p (m u) -> p m u", u=SLOTS)
             turned = bank[:].rearrange("p (u m) -> p m u", u=SLOTS)
@@ -260,39 +266,39 @@ def tile_mask_dice_matching_k5_kernel(
                 nc.scalar.copy(out=dealt, in_=turned)
             else:
                 nc.vector.tensor_copy(out=dealt, in_=turned)
-            nc.sync.dma_start(out=out_0[HALF * h + P * c : HALF * h + P * (c + 1), :], in_=rows[:])
+            queue.dma_start(out=out_0[HALF * h + P * c : HALF * h + P * (c + 1), :], in_=rows[:])
 
         nc.vector.memset(f_scales_first[:].bitcast(I32), 0)
         nc.vector.memset(e_scales[:].bitcast(I32), 0)
         nc.vector.memset(warm[:], 0.0)
         nc.vector.memset(f_scales_rest[:].bitcast(I32), 0)
-        nc.scalar.activation(out=warm_out[:], in_=warm[:], func=ACT.Sigmoid)
-        load_e(0)
-        load_f(0)
         for quadrant in range(4):
             load_scale_rows(nc.sync, f_scales_first, pixel_scales[0, :, :FIRST], quadrant)
-        for quadrant in range(2):
+        load_f(0, nc.scalar)
+        load_e(0, nc.scalar)
+        nc.scalar.activation(out=warm_out[:], in_=warm[:], func=ACT.Sigmoid)
+        for quadrant in range(4):
             load_scale_rows(nc.sync, e_scales, query_scales[0], quadrant)
-        for quadrant in range(2, 4):
-            load_scale_rows(nc.gpsimd, e_scales, query_scales[0], quadrant)
-        nc.gpsimd.dma_start(out=w_raw[:], in_=pixel_weight.rearrange("(g k) -> g k", g=PASSES))
-        load_f(1)
+        nc.sync.dma_start(out=w_raw[:], in_=pixel_weight.rearrange("(g k) -> g k", g=PASSES))
+        load_t(0)
+        load_f(1, nc.sync)
         for quadrant in range(4):
             load_scale_rows(nc.sync, f_scales_rest, pixel_scales[0, :, FIRST:], quadrant)
-        load_t(0)
         load_t(1)
-        load_f(2)
         load_t(2)
-        load_e(1)
+        load_f(2, nc.sync)
+        load_e(1, nc.sync)
         nc.sync.dma_start(out=consts_raw[:, 0, :SLOTS], in_=target_area.rearrange("(p u) -> p u", u=SLOTS))
         nc.sync.dma_start(out=consts_raw[:, 1, :SLOTS], in_=target_gain.rearrange("(p u) -> p u", u=SLOTS))
         for g in range(3, PASSES):
             load_t(g)
-        make_identity(nc, ident[:])
+        nc.vector.memset(ident[:], 0.0)
+        make_identity(nc, ident[:], nomemset=True)
         nc.vector.memset(w_rows[:], 0.0)
         nc.vector.memset(frame_scales4[:], 0)
 
-        deal_f(0)
+        deal_f_codes(0)
+        deal_f_scales(0)
         nc.vector.tensor_copy(
             out=w_rows[:PASSES].rearrange("g t (a e) -> g t a e", e=4),
             in_=w_raw[:].rearrange("g (a t e) -> g t a e", t=SLOTS, e=4),
@@ -303,12 +309,13 @@ def tile_mask_dice_matching_k5_kernel(
 
         for t in range(SLOTS):
             logits(0, t, bank_of(0, t))
+        group_t(0, "vector")
+        deal_f_codes(1)
         for t in range(SLOTS):
-            nc.tensor.transpose(w_bank[:, P * t : P * (t + 1)], w_rows[:, t, :], ident[:])
-        nc.vector.tensor_copy(
-            out=w_cols[:].rearrange("p (g t) -> p g t", t=SLOTS),
-            in_=w_bank[:].rearrange("p (t g) -> p g t", t=SLOTS)[:, :PASSES, :],
-        )
+            nc.tensor.transpose(w_bank[:].rearrange("p (g t) -> p t g", t=SLOTS)[:, t, :], w_rows[:, t, :], ident[:])
+        nc.vector.tensor_copy(out=w_cols[:], in_=w_bank[:, : PASSES * SLOTS])
+        group_t(1, "pool")
+        group_t(2, "pool")
         for s in range(1, LEAD):
             for t in range(SLOTS):
                 logits(s, t, bank_of(s, t))
@@ -338,7 +345,7 @@ def tile_mask_dice_matching_k5_kernel(
         for i in range(STEPS):
             ahead = i + LEAD
             if i == 0:
-                deal_f(1)
+                deal_f_scales(1)
             if i < MID:
                 logits_step(ahead, i - LAG if i >= LAG else None)
             if i == MID - 1:
@@ -373,21 +380,16 @@ def tile_mask_dice_matching_k5_kernel(
             if i == STEPS - 1:
                 load_root_table()
             if i == STEPS - 1:
-                quantize_h(i - 1)
+                quantize(i - 1)
                 areas_upto(i - 1)
                 intersect_step(i - 1)
             weigh(i)
-            if i == 0:
-                group_t(0, "vector")
-            if 1 <= i < STEPS - 1:
-                quantize_h(i - 1)
-            if 1 <= i <= PASSES:
-                quantize_t(i - 1)
             if 1 <= i < PASSES:
                 group_t(i, "vector")
-            if i == 1:
-                deal_f(2)
             if i == 2:
+                deal_f_codes(2)
+                deal_f_scales(2)
+            if i == 1:
                 nc.vector.tensor_copy(out=consts[:], in_=consts_raw[:, :, :SLOTS])
             if i == 3:
                 group_frame()
@@ -395,6 +397,10 @@ def tile_mask_dice_matching_k5_kernel(
                 quantize_frame()
             if i == 5:
                 spread_frame()
+            if 1 <= i < STEPS - 1:
+                quantize(i - 1)
+            if 1 <= i < PASSES - 2:
+                group_t(i + 2, "pool")
             if i == MID + 1:
                 for u in range(SLOTS):
                     ratio(u, whole)
@@ -407,7 +413,7 @@ def tile_mask_dice_matching_k5_kernel(
                 quantize_y(0, whole)
                 store_codes(0)
 
-        quantize_h(STEPS - 1)
+        quantize(STEPS - 1)
         areas_upto(STEPS - 1)
         intersect_step(STEPS - 1)
         free = [bank for bank in logit_bank if bank is not last_area_bank]
@@ -436,9 +442,9 @@ def tile_mask_dice_matching_k5_kernel(
         store_rows(1, 2, tail_banks[2], "scalar")
         quantize_y(1, second)
         store_codes(1)
-        store_rows(1, 3, tail_banks[3], "scalar")
+        store_rows(1, 3, tail_banks[3], "scalar", nc.scalar)
         for quadrant in range(4):
-            nc.sync.dma_start(
+            (nc.sync if quadrant < 2 else nc.scalar).dma_start(
                 out=out_2[0, 4 * quadrant : 4 * quadrant + 4, :].bitcast(I32),
                 in_=y_scales[32 * quadrant : 32 * quadrant + 4, :].bitcast(I32),
             )

@@ -18,21 +18,27 @@ ALU = mybir.AluOpType
 
 P = 128
 SLOTS = 4
+QUADRANTS = 4
 K_PASS = P * SLOTS
 PASSES = PIXELS // K_PASS
 HALF = 512
 HALVES = QUERIES // HALF
 STEPS = HALVES * PASSES
+GROUPED = SLOTS * HALF
+
 F_CHUNKS = ((0, 2), (2, 5), (5, 8))
-FIRST = F_CHUNKS[0][1] * K_PASS
+F_FIRST = F_CHUNKS[0][1] * K_PASS
+LOGIT_BANKS = 3
 SIG_RING = 4
+GROUP_RING = 3
 LEAD = 2
 LAG = 3
-RING = 3
-T_POOL = 24
-T_SCALAR = 32
-T_HEAD = 1
-OUT_RING = 4
+RUNS = TARGETS // 8
+POOL_RUNS = 28
+SCALAR_RUNS = 28
+INVERT_AT = PASSES + 1
+FRAME_AT = 3
+AREAS_FROM = PASSES - 1
 
 
 def tile_mask_dice_matching_k5_kernel(
@@ -45,27 +51,25 @@ def tile_mask_dice_matching_k5_kernel(
         ps = ctx.enter_context(tc.psum_pool(name="ps", bufs=1))
         ctx.enter_context(tc.manual_schedule())
 
-        def tiles(name, count, shape, dtype):
-            return [sb.tile(shape, dtype, name="%s%d" % (name, n), align_bytes=64) for n in range(count)]
-
         def one(name, shape, dtype):
             return sb.tile(shape, dtype, name=name, align_bytes=64)
+
+        def tiles(name, count, shape, dtype):
+            return [one("%s%d" % (name, n), shape, dtype) for n in range(count)]
 
         e_codes = tiles("e_codes", HALVES, [P, 2 * HALF], U8)
         e_scales = one("e_scales", [P, QUERIES], U8)
         f_raw = [one("f_raw%d" % a, [P, (b - a) * K_PASS // 2], I32) for a, b in F_CHUNKS]
-        f_scales_first = one("f_scales_first", [P, FIRST], U8)
-        f_scales_rest = one("f_scales_rest", [P, PIXELS - FIRST], U8)
+        f_scales_first = one("f_scales_first", [P, F_FIRST], U8)
+        f_scales_rest = one("f_scales_rest", [P, PIXELS - F_FIRST], U8)
         f_codes = [one("f_codes%d" % a, [P, (b - a) * K_PASS * 2], U8) for a, b in F_CHUNKS]
         f_scales = [one("f_scales%d" % a, [P, (b - a) * K_PASS], U8) for a, b in F_CHUNKS]
         w_raw = one("w_raw", [PASSES, K_PASS], BF16)
         w_rows = one("w_rows", [P, SLOTS, P], F32)
         w_cols = one("w_cols", [P, PASSES * SLOTS], F32)
         ident = one("ident", [P, P], F32)
-        consts_raw = one("consts_raw", [P, 2, 16], BF16)
-        consts = one("consts", [P, 2, SLOTS], F32)
-        warm = one("warm", [P, 8], F32)
-        warm_out = one("warm_out", [P, 8], F32)
+        area_cols = one("area_cols", [P, SLOTS], BF16)
+        gain_cols = one("gain_cols", [P, SLOTS], BF16)
         t_raw = tiles("t_raw", PASSES, [P, SLOTS, TARGETS], BF16)
         frame_grouped = one("frame_grouped", [P, PASSES, 4, SLOTS], BF16)
         frame_codes4 = one("frame_codes4", [P, PASSES * 4], I32)
@@ -73,23 +77,25 @@ def tile_mask_dice_matching_k5_kernel(
         frame_codes = one("frame_codes", [P, PASSES, P], I32)
         frame_scales = one("frame_scales", [P, PASSES * P], U8)
         sig = tiles("sig", SIG_RING, [P, SLOTS * HALF], F32)
-        grouped = [g[:].rearrange("p (a c) -> p a c", a=2) for g in tiles("grouped", RING, [P, 2 * SLOTS * HALF], BF16)]
+        grouped = tiles("grouped", GROUP_RING, [P, 2 * GROUPED], BF16)
         codes = [one("codes%d" % s, [P, 2 * HALF if s < PASSES else HALF], U32) for s in range(STEPS)]
         scales = [one("scales%d" % s, [P, 2 * HALF if s < PASSES else HALF], U8) for s in range(STEPS)]
-        rsq = tiles("rsq", SLOTS, [P, HALF], F32)
-        inv = tiles("inv", SLOTS, [P, HALF], F32)
+        inv_root = tiles("inv_root", SLOTS, [P, HALF], F32)
+        inverse = tiles("inverse", SLOTS, [P, HALF], F32)
         y_t = one("y_t", [P, SLOTS * HALF], F32)[:].rearrange("p (u c) -> p u c", u=SLOTS)
-        y_grouped = one("y_grouped", [P, HALF * SLOTS], BF16)[:].rearrange("p (c u) -> p c u", u=SLOTS)
+        y_grouped = one("y_grouped", [P, GROUPED], BF16)[:].rearrange("p (c u) -> p c u", u=SLOTS)
         y_codes = tiles("y_codes", HALVES, [P, HALF], U32)
         y_scales = one("y_scales", [P, QUERIES], U8)
-        y_rows = tiles("y_rows", OUT_RING, [P, TARGETS], F32)
+        y_rows = tiles("y_rows", HALF // P, [P, TARGETS], F32)
 
-        logit_bank = [ps.tile([P, 512], F32, name="logit%d" % n) for n in range(3)]
-        w_bank = ps.tile([P, 512], F32, name="w_bank")
-        acc = [ps.tile([P, 512], F32, name="acc%d" % n) for n in range(SLOTS)]
+        logit_banks = [ps.tile([P, 512], F32, name="logit%d" % n) for n in range(LOGIT_BANKS)]
+        side_bank = ps.tile([P, 512], F32, name="side_bank")
+        acc = [ps.tile([P, 512], F32, name="acc%d" % u) for u in range(SLOTS)]
 
-        def chunk_of(g):
-            return [n for n, (a, b) in enumerate(F_CHUNKS) if a <= g < b][0]
+        def logit_bank(s, t):
+            return logit_banks[(SLOTS * s + t) % LOGIT_BANKS]
+
+        last_area_bank = logit_bank(STEPS - 1, SLOTS - LOGIT_BANKS)
 
         def load_scale_rows(queue, plane, rows, quadrant):
             queue.dma_start(
@@ -98,18 +104,19 @@ def tile_mask_dice_matching_k5_kernel(
             )
 
         def load_e(h, queue):
-            queue.dma_start(out=e_codes[h][:].bitcast(I32),
-                              in_=query_words[0, :, 2 * HALF * h : 2 * HALF * (h + 1)].bitcast(I32))
+            queue.dma_start(
+                out=e_codes[h][:].bitcast(I32),
+                in_=query_words[0, :, 2 * HALF * h : 2 * HALF * (h + 1)].bitcast(I32),
+            )
 
         def load_f(n, queue):
             a, b = F_CHUNKS[n]
             queue.dma_start(out=f_raw[n][:], in_=pixel_words[0, :, 2 * K_PASS * a : 2 * K_PASS * b].bitcast(I32))
 
-        t_view = target_masks.rearrange("(g a t e) c -> g e a t c", g=PASSES, t=SLOTS, e=4)
-
         def load_t(g):
+            rows = target_masks.rearrange("(g a t e) c -> g e a t c", g=PASSES, t=SLOTS, e=4)
             for e in range(4):
-                nc.sync.dma_start(out=t_raw[g][e:P:4, :, :], in_=t_view[g, e])
+                nc.sync.dma_start(out=t_raw[g][e:P:4, :, :], in_=rows[g, e])
 
         def deal_f_codes(n):
             nc.vector.tensor_copy(
@@ -119,16 +126,17 @@ def tile_mask_dice_matching_k5_kernel(
 
         def deal_f_scales(n):
             a, b = F_CHUNKS[n]
-            raw_scales = f_scales_first[:] if n == 0 else f_scales_rest[:, K_PASS * a - FIRST : K_PASS * b - FIRST]
+            raw = f_scales_first[:] if n == 0 else f_scales_rest[:, K_PASS * a - F_FIRST : K_PASS * b - F_FIRST]
             nc.vector.tensor_copy(
                 out=f_scales[n][:].bitcast(I32).rearrange("p (g t a i) -> p g a t i", t=SLOTS, a=8, i=4),
-                in_=raw_scales.bitcast(I32).rearrange("p (g a i t) -> p g a t i", t=SLOTS, a=8, i=4),
+                in_=raw.bitcast(I32).rearrange("p (g a i t) -> p g a t i", t=SLOTS, a=8, i=4),
             )
 
-        def logits(s, t, bank):
+        def logits(s, t):
             h, g = divmod(s, PASSES)
-            n = chunk_of(g)
+            n = [a <= g < b for a, b in F_CHUNKS].index(True)
             col = ((g - F_CHUNKS[n][0]) * SLOTS + t) * P
+            bank = logit_bank(s, t)
             nc.tensor.matmul_mx(
                 out=bank[:],
                 lhsT=f_codes[n][:, 2 * col : 2 * (col + P)].bitcast(FP4X4),
@@ -141,34 +149,40 @@ def tile_mask_dice_matching_k5_kernel(
 
         def weigh(s):
             g = s % PASSES
-            weights = w_bank if s < PASSES - 1 and T_POOL else w_cols
+            weights = side_bank if s < PASSES - 1 else w_cols
             nc.vector.tensor_tensor(
-                out=grouped[s % RING][:, 0, :].rearrange("p (c i t) -> p c t i", i=2, t=SLOTS),
+                out=grouped[s % GROUP_RING][:, :GROUPED].rearrange("p (c i t) -> p c t i", i=2, t=SLOTS),
                 in0=sig[s % SIG_RING][:].rearrange("p (t c i) -> p c t i", i=2, t=SLOTS),
                 in1=weights[:, SLOTS * g : SLOTS * (g + 1)].unsqueeze(1).unsqueeze(3).to_broadcast([P, HALF // 2, SLOTS, 2]),
                 op=ALU.mult,
             )
 
         def quantize(s):
-            src = grouped[s % RING][:].rearrange("p a c -> p (a c)") if s < PASSES else grouped[s % RING][:, 0, :]
-            nc.vector.quantize_mx(out=codes[s][:].bitcast(FP8X4), scales=scales[s][:], in_=src)
+            width = 2 * GROUPED if s < PASSES else GROUPED
+            nc.vector.quantize_mx(
+                out=codes[s][:].bitcast(FP8X4), scales=scales[s][:], in_=grouped[s % GROUP_RING][:, :width]
+            )
 
-        def group_t(g, engine):
-            dst = grouped[g % RING][:, 1, :].rearrange("p (u k i j) -> p k u j i", u=SLOTS, i=2, j=SLOTS)
+        def target_runs(g, runs):
+            dst = grouped[g % GROUP_RING][:, GROUPED:].rearrange("p (u k i j) -> p k u j i", u=SLOTS, i=2, j=SLOTS)
             src = t_raw[g][:].rearrange("p j (k i u) -> p k u j i", u=SLOTS, i=2)
-            share = T_POOL + T_SCALAR if g >= T_HEAD else 0
-            if engine == "vector":
-                if share < 64:
-                    nc.vector.tensor_copy(out=dst[:, share:], in_=src[:, share:])
-            elif engine == "scalar":
-                if share:
-                    nc.scalar.copy(out=dst[:, T_POOL:share], in_=src[:, T_POOL:share])
-            elif T_POOL:
-                nc.gpsimd.tensor_scalar(
-                    out=grouped[g % RING][:, 1, :].rearrange("p (u m j) -> p u m j", u=SLOTS, j=SLOTS)[:, :, : 2 * T_POOL],
-                    in0=t_raw[g][:].rearrange("p j (m u) -> p u m j", u=SLOTS)[:, :, : 2 * T_POOL],
-                    scalar1=1.0, scalar2=0.0, op0=ALU.mult, op1=ALU.add,
-                )
+            return dst[:, runs], src[:, runs]
+
+        def group_targets_vector(g, first_run):
+            dst, src = target_runs(g, slice(first_run, RUNS))
+            nc.vector.tensor_copy(out=dst, in_=src)
+
+        def group_targets_scalar(g):
+            dst, src = target_runs(g, slice(POOL_RUNS, POOL_RUNS + SCALAR_RUNS))
+            nc.scalar.copy(out=dst, in_=src)
+
+        def group_targets_pool(g):
+            dst = grouped[g % GROUP_RING][:, GROUPED:].rearrange("p (u m j) -> p u m j", u=SLOTS, j=SLOTS)
+            src = t_raw[g][:].rearrange("p j (m u) -> p u m j", u=SLOTS)
+            nc.gpsimd.tensor_scalar(
+                out=dst[:, :, : 2 * POOL_RUNS], in0=src[:, :, : 2 * POOL_RUNS],
+                scalar1=1.0, scalar2=0.0, op0=ALU.mult, op1=ALU.add,
+            )
 
         def group_frame():
             for g in range(PASSES):
@@ -178,8 +192,10 @@ def tile_mask_dice_matching_k5_kernel(
                 )
 
         def quantize_frame():
-            nc.vector.quantize_mx(out=frame_codes4[:].bitcast(FP8X4), scales=frame_scales4[:],
-                                  in_=frame_grouped[:].rearrange("p g c j -> p (g c j)"))
+            nc.vector.quantize_mx(
+                out=frame_codes4[:].bitcast(FP8X4), scales=frame_scales4[:],
+                in_=frame_grouped[:].rearrange("p g c j -> p (g c j)"),
+            )
 
         def spread_frame():
             nc.vector.tensor_copy(
@@ -193,54 +209,64 @@ def tile_mask_dice_matching_k5_kernel(
 
         def intersect(s, u):
             g = s % PASSES
+            cols = slice(HALF + P * u, HALF + P * (u + 1))
             nc.tensor.matmul_mx(
                 out=acc[u][:],
-                lhsT=codes[g][:, HALF + P * u : HALF + P * (u + 1)].bitcast(FP8X4),
-                lhsT_scale=scales[g][:, HALF + P * u : HALF + P * (u + 1)],
+                lhsT=codes[g][:, cols].bitcast(FP8X4), lhsT_scale=scales[g][:, cols],
                 rhs=codes[s][:, :HALF].bitcast(FP8X4), rhs_scale=scales[s][:, :HALF],
                 start=(g == 0), stop=(g == PASSES - 1),
             )
 
-        def predicted_area(s, bank):
-            g = s % PASSES
-            nc.tensor.matmul_mx(
-                out=bank[:],
-                lhsT=frame_codes[:, g, :].bitcast(FP8X4),
-                lhsT_scale=frame_scales[:, P * g : P * (g + 1)],
-                rhs=codes[s][:, :HALF].bitcast(FP8X4), rhs_scale=scales[s][:, :HALF],
-                start=(g == 0), stop=(g == PASSES - 1),
+        def intersect_step(s):
+            for u in range(SLOTS):
+                intersect(s, u)
+
+        def predicted_areas(steps):
+            for s in steps:
+                g = s % PASSES
+                bank = side_bank if s < PASSES else last_area_bank
+                nc.tensor.matmul_mx(
+                    out=bank[:],
+                    lhsT=frame_codes[:, g, :].bitcast(FP8X4), lhsT_scale=frame_scales[:, P * g : P * (g + 1)],
+                    rhs=codes[s][:, :HALF].bitcast(FP8X4), rhs_scale=scales[s][:, :HALF],
+                    start=(g == 0), stop=(g == PASSES - 1),
+                )
+
+        def logits_among_intersections(s, earlier):
+            for t in range(SLOTS):
+                logits(s, t)
+                intersect(earlier, t)
+
+        def invert_root(u, bank, cols):
+            nc.scalar.activation(
+                out=inv_root[u][:, cols], in_=bank[:, cols], func=ACT.Abs_reciprocal_sqrt, bias=area_cols[:, u : u + 1]
             )
 
-        def inverse_root(u, bank, cols):
-            nc.scalar.activation(out=rsq[u][:, cols], in_=bank[:, cols], func=ACT.Abs_reciprocal_sqrt, bias=consts[:, 0, u : u + 1])
+        def square_scalar(u, cols):
+            nc.scalar.activation(out=inverse[u][:, cols], in_=inv_root[u][:, cols], func=ACT.Square)
 
-        def square(u, cols, engine):
-            if engine == "scalar":
-                nc.scalar.activation(out=inv[u][:, cols], in_=rsq[u][:, cols], func=ACT.Square)
-            else:
-                nc.vector.tensor_tensor(out=inv[u][:, cols], in0=rsq[u][:, cols], in1=rsq[u][:, cols], op=ALU.mult)
-
-        def load_root_table():
-            nc.scalar.activation(out=warm_out[:], in_=ident[:, :8], func=ACT.Abs_reciprocal_sqrt, bias=1.0)
+        def square_vector(u, cols):
+            nc.vector.tensor_tensor(
+                out=inverse[u][:, cols], in0=inv_root[u][:, cols], in1=inv_root[u][:, cols], op=ALU.mult
+            )
 
         def ratio(u, cols):
             nc.vector.scalar_tensor_tensor(
-                out=y_t[:, u, cols], in0=acc[u][:, cols], scalar=consts[:, 1, u : u + 1],
-                in1=inv[u][:, cols], op0=ALU.mult, op1=ALU.mult,
+                out=y_t[:, u, cols], in0=acc[u][:, cols], scalar=gain_cols[:, u : u + 1],
+                in1=inverse[u][:, cols], op0=ALU.mult, op1=ALU.mult,
             )
 
-        def group_y(cols, engine):
+        def y_views(cols):
             dst = y_grouped[:, cols, :].rearrange("p (c i) u -> p c u i", i=2)
             src = y_t[:, :, cols].rearrange("p u (c i) -> p c u i", i=2)
-            if engine == "scalar":
-                nc.scalar.copy(out=dst, in_=src)
-            else:
-                nc.vector.tensor_copy(out=dst, in_=src)
+            return dst, src
 
         def quantize_y(h, cols):
-            out_cols = slice(HALF * h + cols.start, HALF * h + cols.stop)
-            nc.vector.quantize_mx(out=y_codes[h][:, cols].bitcast(FP8X4), scales=y_scales[:, out_cols],
-                                  in_=y_grouped[:, cols, :].rearrange("p c u -> p (c u)"))
+            nc.vector.quantize_mx(
+                out=y_codes[h][:, cols].bitcast(FP8X4),
+                scales=y_scales[:, HALF * h + cols.start : HALF * h + cols.stop],
+                in_=y_grouped[:, cols, :].rearrange("p c u -> p (c u)"),
+            )
 
         def store_codes(h):
             nc.sync.dma_start(
@@ -248,48 +274,40 @@ def tile_mask_dice_matching_k5_kernel(
                 in_=y_codes[h][:].bitcast(I32),
             )
 
-        def turn_one(c, u, bank):
-            nc.tensor.transpose(
-                bank[:, P * u : P * (u + 1)],
-                y_t[:, u, P * c : P * (c + 1)], ident[:],
-            )
-
         def turn(c, bank):
             for u in range(SLOTS):
-                turn_one(c, u, bank)
+                nc.tensor.transpose(bank[:, P * u : P * (u + 1)], y_t[:, u, P * c : P * (c + 1)], ident[:])
 
-        def store_rows(h, c, bank, engine, queue=nc.sync):
-            rows = y_rows[c % OUT_RING]
-            dealt = rows[:].rearrange("p (m u) -> p m u", u=SLOTS)
-            turned = bank[:].rearrange("p (u m) -> p m u", u=SLOTS)
-            if engine == "scalar":
-                nc.scalar.copy(out=dealt, in_=turned)
-            else:
-                nc.vector.tensor_copy(out=dealt, in_=turned)
-            queue.dma_start(out=out_0[HALF * h + P * c : HALF * h + P * (c + 1), :], in_=rows[:])
+        def store_rows(h, c, bank, queue):
+            nc.scalar.copy(
+                out=y_rows[c][:].rearrange("p (m u) -> p m u", u=SLOTS),
+                in_=bank[:].rearrange("p (u m) -> p m u", u=SLOTS),
+            )
+            queue.dma_start(out=out_0[HALF * h + P * c : HALF * h + P * (c + 1), :], in_=y_rows[c][:])
+
+        whole = slice(0, HALF)
+        first, second = slice(0, HALF // 2), slice(HALF // 2, HALF)
 
         nc.vector.memset(f_scales_first[:].bitcast(I32), 0)
         nc.vector.memset(e_scales[:].bitcast(I32), 0)
-        nc.vector.memset(warm[:], 0.0)
         nc.vector.memset(f_scales_rest[:].bitcast(I32), 0)
-        for quadrant in range(4):
-            load_scale_rows(nc.sync, f_scales_first, pixel_scales[0, :, :FIRST], quadrant)
+        for quadrant in range(QUADRANTS):
+            load_scale_rows(nc.sync, f_scales_first, pixel_scales[0, :, :F_FIRST], quadrant)
         load_f(0, nc.scalar)
         load_e(0, nc.scalar)
-        nc.scalar.activation(out=warm_out[:], in_=warm[:], func=ACT.Sigmoid)
-        for quadrant in range(4):
-            load_scale_rows(nc.sync, e_scales, query_scales[0], quadrant)
+        for quadrant in range(QUADRANTS):
+            load_scale_rows(nc.sync if quadrant < QUADRANTS - 1 else nc.gpsimd, e_scales, query_scales[0], quadrant)
         nc.sync.dma_start(out=w_raw[:], in_=pixel_weight.rearrange("(g k) -> g k", g=PASSES))
         load_t(0)
         load_f(1, nc.sync)
-        for quadrant in range(4):
-            load_scale_rows(nc.sync, f_scales_rest, pixel_scales[0, :, FIRST:], quadrant)
+        for quadrant in range(QUADRANTS):
+            load_scale_rows(nc.sync, f_scales_rest, pixel_scales[0, :, F_FIRST:], quadrant)
         load_t(1)
         load_t(2)
         load_f(2, nc.sync)
         load_e(1, nc.sync)
-        nc.sync.dma_start(out=consts_raw[:, 0, :SLOTS], in_=target_area.rearrange("(p u) -> p u", u=SLOTS))
-        nc.sync.dma_start(out=consts_raw[:, 1, :SLOTS], in_=target_gain.rearrange("(p u) -> p u", u=SLOTS))
+        nc.sync.dma_start(out=area_cols[:], in_=target_area.rearrange("(p u) -> p u", u=SLOTS))
+        nc.sync.dma_start(out=gain_cols[:], in_=target_gain.rearrange("(p u) -> p u", u=SLOTS))
         for g in range(3, PASSES):
             load_t(g)
         nc.vector.memset(ident[:], 0.0)
@@ -303,148 +321,123 @@ def tile_mask_dice_matching_k5_kernel(
             out=w_rows[:PASSES].rearrange("g t (a e) -> g t a e", e=4),
             in_=w_raw[:].rearrange("g (a t e) -> g t a e", t=SLOTS, e=4),
         )
-
-        def bank_of(s, t):
-            return logit_bank[(SLOTS * s + t) % 3]
-
         for t in range(SLOTS):
-            logits(0, t, bank_of(0, t))
-        group_t(0, "vector")
+            logits(0, t)
+        group_targets_vector(0, 0)
         deal_f_codes(1)
         for t in range(SLOTS):
-            nc.tensor.transpose(w_bank[:].rearrange("p (g t) -> p t g", t=SLOTS)[:, t, :], w_rows[:, t, :], ident[:])
-        nc.vector.tensor_copy(out=w_cols[:], in_=w_bank[:, : PASSES * SLOTS])
-        group_t(1, "pool")
-        group_t(2, "pool")
-        for s in range(1, LEAD):
-            for t in range(SLOTS):
-                logits(s, t, bank_of(s, t))
-
-        MID = PASSES + 1
-        spare = w_bank
-        whole = slice(0, HALF)
-        first, second = slice(0, HALF // 2), slice(HALF // 2, HALF)
-        areas = [0]
-        last_area_bank = bank_of(STEPS - 1, 1)
-
-        def areas_upto(s):
-            while areas[0] <= s:
-                predicted_area(areas[0], spare if areas[0] < PASSES else last_area_bank)
-                areas[0] = areas[0] + 1
-
-        def intersect_step(s):
-            for u in range(SLOTS):
-                intersect(s, u)
-
-        def logits_step(s, back):
-            for t in range(SLOTS):
-                logits(s, t, bank_of(s, t))
-                if back is not None:
-                    intersect(back, t)
+            nc.tensor.transpose(side_bank[:].rearrange("p (g t) -> p t g", t=SLOTS)[:, t, :], w_rows[:, t, :], ident[:])
+        nc.vector.tensor_copy(out=w_cols[:], in_=side_bank[:, : PASSES * SLOTS])
+        for g in range(1, GROUP_RING):
+            group_targets_pool(g)
+        for t in range(SLOTS):
+            logits(1, t)
+        deal_f_scales(1)
 
         for i in range(STEPS):
             ahead = i + LEAD
-            if i == 0:
-                deal_f_scales(1)
-            if i < MID:
-                logits_step(ahead, i - LAG if i >= LAG else None)
-            if i == MID - 1:
-                logits_step(ahead + 1, i + 1 - LAG)
-            if i < PASSES:
-                group_t(i, "scalar")
-            if 6 < i < MID:
-                areas_upto(min(4 * (i - 6) - 1, i - 2))
-            if i == MID:
-                load_root_table()
-                areas_upto(PASSES - 1)
+
+            if i < LAG:
+                for t in range(SLOTS):
+                    logits(ahead, t)
+            elif i < INVERT_AT:
+                logits_among_intersections(ahead, i - LAG)
+            if i == INVERT_AT - 1:
+                logits_among_intersections(ahead + 1, i + 1 - LAG)
+            if 1 <= i < PASSES:
+                group_targets_scalar(i)
+            if i == AREAS_FROM:
+                predicted_areas(range(0, PASSES // 2))
+            if i == AREAS_FROM + 1:
+                predicted_areas(range(PASSES // 2, PASSES - 1))
+            if i == INVERT_AT:
+                predicted_areas([PASSES - 1])
                 intersect_step(PASSES - 1)
-                for u in range(SLOTS + 1):
-                    if u < SLOTS:
-                        inverse_root(u, spare, whole)
+                for u in range(SLOTS):
+                    invert_root(u, side_bank, whole)
                     if u >= 1:
-                        square(u - 1, whole, "scalar")
-            if i == MID + 1:
-                for t in range(SLOTS - 1):
-                    logits(ahead, t, bank_of(ahead, t))
-            if MID + 1 < i and ahead < STEPS:
-                logits_step(ahead, i - 2)
-            if MID + 2 <= i < MID + 1 + SLOTS:
-                turn(i - MID - 1, spare)
-                store_rows(0, i - MID - 1, spare, "scalar")
+                        square_scalar(u - 1, whole)
+                square_scalar(SLOTS - 1, whole)
+            if i == INVERT_AT + 1:
+                for t in range(LOGIT_BANKS):
+                    logits(ahead, t)
+            if INVERT_AT + 1 < i and ahead < STEPS:
+                logits_among_intersections(ahead, i - 2)
+                turn(i - INVERT_AT - 1, side_bank)
+                store_rows(0, i - INVERT_AT - 1, side_bank, nc.sync)
             if ahead == STEPS - 1:
-                group_y(whole, "scalar")
+                dst, src = y_views(whole)
+                nc.scalar.copy(out=dst, in_=src)
+            if ahead == STEPS:
+                predicted_areas(range(PASSES, i - 2))
             if ahead >= STEPS:
-                areas_upto(i - 3)
                 intersect_step(i - 2)
-                areas_upto(i - 2)
-            if i == STEPS - 1:
-                load_root_table()
+                predicted_areas([i - 2])
+
             if i == STEPS - 1:
                 quantize(i - 1)
-                areas_upto(i - 1)
+                predicted_areas([i - 1])
                 intersect_step(i - 1)
             weigh(i)
             if 1 <= i < PASSES:
-                group_t(i, "vector")
+                group_targets_vector(i, POOL_RUNS + SCALAR_RUNS)
             if i == 2:
                 deal_f_codes(2)
                 deal_f_scales(2)
-            if i == 1:
-                nc.vector.tensor_copy(out=consts[:], in_=consts_raw[:, :, :SLOTS])
-            if i == 3:
+            if i == FRAME_AT:
                 group_frame()
-            if i == 4:
+            if i == FRAME_AT + 1:
                 quantize_frame()
-            if i == 5:
+            if i == FRAME_AT + 2:
                 spread_frame()
             if 1 <= i < STEPS - 1:
                 quantize(i - 1)
-            if 1 <= i < PASSES - 2:
-                group_t(i + 2, "pool")
-            if i == MID + 1:
+            if 1 <= i and i - 1 + GROUP_RING < PASSES:
+                group_targets_pool(i - 1 + GROUP_RING)
+            if i == INVERT_AT + 1:
                 for u in range(SLOTS):
                     ratio(u, whole)
                     intersect(PASSES, u)
                     if u == 1:
-                        logits(ahead, SLOTS - 1, bank_of(ahead, SLOTS - 1))
-                turn(0, spare)
-                store_rows(0, 0, spare, "scalar")
-            if i == STEPS - 1:
-                quantize_y(0, whole)
-                store_codes(0)
+                        logits(ahead, SLOTS - 1)
+                turn(0, side_bank)
+                store_rows(0, 0, side_bank, nc.sync)
 
         quantize(STEPS - 1)
-        areas_upto(STEPS - 1)
+        predicted_areas([STEPS - 1])
         intersect_step(STEPS - 1)
-        free = [bank for bank in logit_bank if bank is not last_area_bank]
-        tail_banks = free + [spare, free[0]]
+        quantize_y(0, whole)
+        store_codes(0)
+        free_banks = [bank for bank in logit_banks if bank is not last_area_bank]
+        turn_banks = free_banks + [side_bank, free_banks[0]]
+        for cols in (first, second):
+            for u in range(SLOTS):
+                invert_root(u, last_area_bank, cols)
         for u in range(SLOTS):
-            inverse_root(u, last_area_bank, first)
-        for u in range(SLOTS):
-            inverse_root(u, last_area_bank, second)
-        for u in range(SLOTS):
-            square(u, first, "vector")
+            square_vector(u, first)
         for u in range(SLOTS):
             ratio(u, first)
         for u in range(SLOTS):
-            square(u, second, "scalar")
-        turn(0, tail_banks[0])
-        turn(1, tail_banks[1])
-        store_rows(1, 0, tail_banks[0], "scalar")
-        store_rows(1, 1, tail_banks[1], "scalar")
+            square_scalar(u, second)
+        for c in (0, 1):
+            turn(c, turn_banks[c])
+        for c in (0, 1):
+            store_rows(1, c, turn_banks[c], nc.sync)
         for u in range(SLOTS):
             ratio(u, second)
-        turn(2, tail_banks[2])
-        turn(3, tail_banks[3])
-        group_y(first, "vector")
-        group_y(second, "vector")
+        for c in (2, 3):
+            turn(c, turn_banks[c])
+        for cols in (first, second):
+            dst, src = y_views(cols)
+            nc.vector.tensor_copy(out=dst, in_=src)
         quantize_y(1, first)
-        store_rows(1, 2, tail_banks[2], "scalar")
+        store_rows(1, 2, turn_banks[2], nc.sync)
         quantize_y(1, second)
         store_codes(1)
-        store_rows(1, 3, tail_banks[3], "scalar", nc.scalar)
-        for quadrant in range(4):
-            (nc.sync if quadrant < 2 else nc.scalar).dma_start(
+        store_rows(1, 3, turn_banks[3], nc.scalar)
+        for quadrant in range(QUADRANTS):
+            queue = nc.sync if quadrant < QUADRANTS // 2 else nc.scalar
+            queue.dma_start(
                 out=out_2[0, 4 * quadrant : 4 * quadrant + 4, :].bitcast(I32),
                 in_=y_scales[32 * quadrant : 32 * quadrant + 4, :].bitcast(I32),
             )

from contextlib import ExitStack

import concourse.mybir as mybir
from concourse.masks import make_identity

QUERIES, CHANNELS, PIXELS, TARGETS = 1024, 512, 4096, 512
FLOPS = 2 * QUERIES * PIXELS * (CHANNELS + TARGETS)

F32 = mybir.dt.float32
BF16 = mybir.dt.bfloat16
I32 = mybir.dt.int32
U32 = mybir.dt.uint32
U8 = mybir.dt.uint8
FP8X4 = mybir.dt.float8_e4m3fn_x4
FP4X4 = mybir.dt.float4_e2m1fn_x4
ACT = mybir.ActivationFunctionType
ALU = mybir.AluOpType

P = 128
SLOTS = 4
QUADRANTS = 4
K_PASS = P * SLOTS
PASSES = PIXELS // K_PASS
HALF = 512
HALVES = QUERIES // HALF
STEPS = HALVES * PASSES
GROUPED = SLOTS * HALF

F_CHUNKS = ((0, 2), (2, 5), (5, 8))
F_FIRST = F_CHUNKS[0][1] * K_PASS
LOGIT_BANKS = 3
SIG_RING = 4
GROUP_RING = 3
LEAD = 2
LAG = 3
RUNS = TARGETS // 8
POOL_RUNS = 28
SCALAR_RUNS = 28
INVERT_AT = PASSES + 1
FRAME_AT = 3
AREAS_FROM = PASSES - 1


def tile_mask_dice_matching_k5_kernel(
    tc, query_words, query_scales, pixel_words, pixel_scales, pixel_weight,
    target_masks, target_area, target_gain, out_0, out_1, out_2,
):
    nc = tc.nc
    with ExitStack() as ctx:
        sb = ctx.enter_context(tc.tile_pool(name="sb", bufs=1))
        ps = ctx.enter_context(tc.psum_pool(name="ps", bufs=1))
        ctx.enter_context(tc.manual_schedule())

        def one(name, shape, dtype):
            return sb.tile(shape, dtype, name=name, align_bytes=64)

        def tiles(name, count, shape, dtype):
            return [one("%s%d" % (name, n), shape, dtype) for n in range(count)]

        e_codes = tiles("e_codes", HALVES, [P, 2 * HALF], U8)
        e_scales = one("e_scales", [P, QUERIES], U8)
        f_raw = [one("f_raw%d" % a, [P, (b - a) * K_PASS // 2], I32) for a, b in F_CHUNKS]
        f_scales_first = one("f_scales_first", [P, F_FIRST], U8)
        f_scales_rest = one("f_scales_rest", [P, PIXELS - F_FIRST], U8)
        f_codes = [one("f_codes%d" % a, [P, (b - a) * K_PASS * 2], U8) for a, b in F_CHUNKS]
        f_scales = [one("f_scales%d" % a, [P, (b - a) * K_PASS], U8) for a, b in F_CHUNKS]
        w_raw = one("w_raw", [PASSES, K_PASS], BF16)
        w_rows = one("w_rows", [P, SLOTS, P], F32)
        w_cols = one("w_cols", [P, PASSES * SLOTS], F32)
        ident = one("ident", [P, P], F32)
        area_cols = one("area_cols", [P, SLOTS], BF16)
        gain_cols = one("gain_cols", [P, SLOTS], BF16)
        t_raw = tiles("t_raw", PASSES, [P, SLOTS, TARGETS], BF16)
        frame_grouped = one("frame_grouped", [P, PASSES, 4, SLOTS], BF16)
        frame_codes4 = one("frame_codes4", [P, PASSES * 4], I32)
        frame_scales4 = one("frame_scales4", [P, PASSES * 4], U8)
        frame_codes = one("frame_codes", [P, PASSES, P], I32)
        frame_scales = one("frame_scales", [P, PASSES * P], U8)
        sig = tiles("sig", SIG_RING, [P, SLOTS * HALF], F32)
        grouped = tiles("grouped", GROUP_RING, [P, 2 * GROUPED], BF16)
        codes = [one("codes%d" % s, [P, 2 * HALF if s < PASSES else HALF], U32) for s in range(STEPS)]
        scales = [one("scales%d" % s, [P, 2 * HALF if s < PASSES else HALF], U8) for s in range(STEPS)]
        inv_root = tiles("inv_root", SLOTS, [P, HALF], F32)
        inverse = tiles("inverse", SLOTS, [P, HALF], F32)
        y_t = one("y_t", [P, SLOTS * HALF], F32)[:].rearrange("p (u c) -> p u c", u=SLOTS)
        y_grouped = one("y_grouped", [P, GROUPED], BF16)[:].rearrange("p (c u) -> p c u", u=SLOTS)
        y_codes = tiles("y_codes", HALVES, [P, HALF], U32)
        y_scales = one("y_scales", [P, QUERIES], U8)
        y_rows = tiles("y_rows", HALF // P, [P, TARGETS], F32)

        logit_banks = [ps.tile([P, 512], F32, name="logit%d" % n) for n in range(LOGIT_BANKS)]
        side_bank = ps.tile([P, 512], F32, name="side_bank")
        acc = [ps.tile([P, 512], F32, name="acc%d" % u) for u in range(SLOTS)]

        def logit_bank(s, t):
            return logit_banks[(SLOTS * s + t) % LOGIT_BANKS]

        last_area_bank = logit_bank(STEPS - 1, SLOTS - LOGIT_BANKS)

        def load_scale_rows(queue, plane, rows, quadrant):
            queue.dma_start(
                out=plane[32 * quadrant : 32 * quadrant + 4, :].bitcast(I32),
                in_=rows[4 * quadrant : 4 * quadrant + 4, :].bitcast(I32),
            )

        def load_e(h, queue):
            queue.dma_start(
                out=e_codes[h][:].bitcast(I32),
                in_=query_words[0, :, 2 * HALF * h : 2 * HALF * (h + 1)].bitcast(I32),
            )

        def load_f(n, queue):
            a, b = F_CHUNKS[n]
            queue.dma_start(out=f_raw[n][:], in_=pixel_words[0, :, 2 * K_PASS * a : 2 * K_PASS * b].bitcast(I32))

        def load_t(g):
            rows = target_masks.rearrange("(g a t e) c -> g e a t c", g=PASSES, t=SLOTS, e=4)
            for e in range(4):
                nc.sync.dma_start(out=t_raw[g][e:P:4, :, :], in_=rows[g, e])

        def deal_f_codes(n):
            nc.vector.tensor_copy(
                out=f_codes[n][:].bitcast(I32).rearrange("p (g t a w) -> p g t a w", t=SLOTS, a=32, w=2),
                in_=f_raw[n][:].rearrange("p (g a t w) -> p g t a w", t=SLOTS, a=32, w=2),
            )

        def deal_f_scales(n):
            a, b = F_CHUNKS[n]
            raw = f_scales_first[:] if n == 0 else f_scales_rest[:, K_PASS * a - F_FIRST : K_PASS * b - F_FIRST]
            nc.vector.tensor_copy(
                out=f_scales[n][:].bitcast(I32).rearrange("p (g t a i) -> p g a t i", t=SLOTS, a=8, i=4),
                in_=raw.bitcast(I32).rearrange("p (g a i t) -> p g a t i", t=SLOTS, a=8, i=4),
            )

        def logits(s, t):
            h, g = divmod(s, PASSES)
            n = [a <= g < b for a, b in F_CHUNKS].index(True)
            col = ((g - F_CHUNKS[n][0]) * SLOTS + t) * P
            bank = logit_bank(s, t)
            nc.tensor.matmul_mx(
                out=bank[:],
                lhsT=f_codes[n][:, 2 * col : 2 * (col + P)].bitcast(FP4X4),
                lhsT_scale=f_scales[n][:, col : col + P],
                rhs=e_codes[h][:].bitcast(FP4X4),
                rhs_scale=e_scales[:, HALF * h : HALF * (h + 1)],
                start=True, stop=True,
            )
            nc.scalar.activation(out=sig[s % SIG_RING][:, HALF * t : HALF * (t + 1)], in_=bank[:], func=ACT.Sigmoid)

        def weigh(s):
            g = s % PASSES
            weights = side_bank if s < PASSES - 1 else w_cols
            nc.vector.tensor_tensor(
                out=grouped[s % GROUP_RING][:, :GROUPED].rearrange("p (c i t) -> p c t i", i=2, t=SLOTS),
                in0=sig[s % SIG_RING][:].rearrange("p (t c i) -> p c t i", i=2, t=SLOTS),
                in1=weights[:, SLOTS * g : SLOTS * (g + 1)].unsqueeze(1).unsqueeze(3).to_broadcast([P, HALF // 2, SLOTS, 2]),
                op=ALU.mult,
            )

        def quantize(s):
            width = 2 * GROUPED if s < PASSES else GROUPED
            nc.vector.quantize_mx(
                out=codes[s][:].bitcast(FP8X4), scales=scales[s][:], in_=grouped[s % GROUP_RING][:, :width]
            )

        def target_runs(g, runs):
            dst = grouped[g % GROUP_RING][:, GROUPED:].rearrange("p (u k i j) -> p k u j i", u=SLOTS, i=2, j=SLOTS)
            src = t_raw[g][:].rearrange("p j (k i u) -> p k u j i", u=SLOTS, i=2)
            return dst[:, runs], src[:, runs]

        def group_targets_vector(g, first_run):
            dst, src = target_runs(g, slice(first_run, RUNS))
            nc.vector.tensor_copy(out=dst, in_=src)

        def group_targets_scalar(g):
            dst, src = target_runs(g, slice(POOL_RUNS, POOL_RUNS + SCALAR_RUNS))
            nc.scalar.copy(out=dst, in_=src)

        def group_targets_pool(g):
            dst = grouped[g % GROUP_RING][:, GROUPED:].rearrange("p (u m j) -> p u m j", u=SLOTS, j=SLOTS)
            src = t_raw[g][:].rearrange("p j (m u) -> p u m j", u=SLOTS)
            nc.gpsimd.tensor_scalar(
                out=dst[:, :, : 2 * POOL_RUNS], in0=src[:, :, : 2 * POOL_RUNS],
                scalar1=1.0, scalar2=0.0, op0=ALU.mult, op1=ALU.add,
            )

        def group_frame():
            for g in range(PASSES):
                nc.scalar.copy(
                    out=frame_grouped[:, g],
                    in_=t_raw[g][:, :, TARGETS - 1].unsqueeze(1).to_broadcast([P, 4, SLOTS]),
                )

        def quantize_frame():
            nc.vector.quantize_mx(
                out=frame_codes4[:].bitcast(FP8X4), scales=frame_scales4[:],
                in_=frame_grouped[:].rearrange("p g c j -> p (g c j)"),
            )

        def spread_frame():
            nc.vector.tensor_copy(
                out=frame_codes[:],
                in_=frame_codes4[:].rearrange("p (g c) -> p g c", c=4)[:, :, 0:1].to_broadcast([P, PASSES, P]),
            )
            nc.vector.tensor_copy(
                out=frame_scales[:].bitcast(I32).rearrange("p (g c) -> p g c", g=PASSES),
                in_=frame_scales4[:].bitcast(I32).unsqueeze(2).to_broadcast([P, PASSES, P // 4]),
            )

        def intersect(s, u):
            g = s % PASSES
            cols = slice(HALF + P * u, HALF + P * (u + 1))
            nc.tensor.matmul_mx(
                out=acc[u][:],
                lhsT=codes[g][:, cols].bitcast(FP8X4), lhsT_scale=scales[g][:, cols],
                rhs=codes[s][:, :HALF].bitcast(FP8X4), rhs_scale=scales[s][:, :HALF],
                start=(g == 0), stop=(g == PASSES - 1),
            )

        def intersect_step(s):
            for u in range(SLOTS):
                intersect(s, u)

        def predicted_areas(steps):
            for s in steps:
                g = s % PASSES
                bank = side_bank if s < PASSES else last_area_bank
                nc.tensor.matmul_mx(
                    out=bank[:],
                    lhsT=frame_codes[:, g, :].bitcast(FP8X4), lhsT_scale=frame_scales[:, P * g : P * (g + 1)],
                    rhs=codes[s][:, :HALF].bitcast(FP8X4), rhs_scale=scales[s][:, :HALF],
                    start=(g == 0), stop=(g == PASSES - 1),
                )

        def logits_among_intersections(s, earlier):
            for t in range(SLOTS):
                logits(s, t)
                intersect(earlier, t)

        def invert_root(u, bank, cols):
            nc.scalar.activation(
                out=inv_root[u][:, cols], in_=bank[:, cols], func=ACT.Abs_reciprocal_sqrt, bias=area_cols[:, u : u + 1]
            )

        def square_scalar(u, cols):
            nc.scalar.activation(out=inverse[u][:, cols], in_=inv_root[u][:, cols], func=ACT.Square)

        def square_vector(u, cols):
            nc.vector.tensor_tensor(
                out=inverse[u][:, cols], in0=inv_root[u][:, cols], in1=inv_root[u][:, cols], op=ALU.mult
            )

        def ratio(u, cols):
            nc.vector.scalar_tensor_tensor(
                out=y_t[:, u, cols], in0=acc[u][:, cols], scalar=gain_cols[:, u : u + 1],
                in1=inverse[u][:, cols], op0=ALU.mult, op1=ALU.mult,
            )

        def y_views(cols):
            dst = y_grouped[:, cols, :].rearrange("p (c i) u -> p c u i", i=2)
            src = y_t[:, :, cols].rearrange("p u (c i) -> p c u i", i=2)
            return dst, src

        def quantize_y(h, cols):
            nc.vector.quantize_mx(
                out=y_codes[h][:, cols].bitcast(FP8X4),
                scales=y_scales[:, HALF * h + cols.start : HALF * h + cols.stop],
                in_=y_grouped[:, cols, :].rearrange("p c u -> p (c u)"),
            )

        def store_codes(h):
            nc.sync.dma_start(
                out=out_1[0, :, HALF * h : HALF * (h + 1), :].rearrange("p m t -> p (m t)").bitcast(I32),
                in_=y_codes[h][:].bitcast(I32),
            )

        def turn(c, bank):
            for u in range(SLOTS):
                nc.tensor.transpose(bank[:, P * u : P * (u + 1)], y_t[:, u, P * c : P * (c + 1)], ident[:])

        def store_rows(h, c, bank, queue):
            nc.scalar.copy(
                out=y_rows[c][:].rearrange("p (m u) -> p m u", u=SLOTS),
                in_=bank[:].rearrange("p (u m) -> p m u", u=SLOTS),
            )
            queue.dma_start(out=out_0[HALF * h + P * c : HALF * h + P * (c + 1), :], in_=y_rows[c][:])

        whole = slice(0, HALF)
        first, second = slice(0, HALF // 2), slice(HALF // 2, HALF)

        nc.vector.memset(f_scales_first[:].bitcast(I32), 0)
        nc.vector.memset(e_scales[:].bitcast(I32), 0)
        nc.vector.memset(f_scales_rest[:].bitcast(I32), 0)
        for quadrant in range(QUADRANTS):
            load_scale_rows(nc.sync, f_scales_first, pixel_scales[0, :, :F_FIRST], quadrant)
        load_f(0, nc.scalar)
        load_e(0, nc.scalar)
        for quadrant in range(QUADRANTS):
            load_scale_rows(nc.sync if quadrant < QUADRANTS - 1 else nc.gpsimd, e_scales, query_scales[0], quadrant)
        nc.sync.dma_start(out=w_raw[:], in_=pixel_weight.rearrange("(g k) -> g k", g=PASSES))
        load_t(0)
        load_f(1, nc.sync)
        for quadrant in range(QUADRANTS):
            load_scale_rows(nc.sync, f_scales_rest, pixel_scales[0, :, F_FIRST:], quadrant)
        load_t(1)
        load_t(2)
        load_f(2, nc.sync)
        load_e(1, nc.sync)
        nc.sync.dma_start(out=area_cols[:], in_=target_area.rearrange("(p u) -> p u", u=SLOTS))
        nc.sync.dma_start(out=gain_cols[:], in_=target_gain.rearrange("(p u) -> p u", u=SLOTS))
        for g in range(3, PASSES):
            load_t(g)
        nc.vector.memset(ident[:], 0.0)
        make_identity(nc, ident[:], nomemset=True)
        nc.vector.memset(w_rows[:], 0.0)
        nc.vector.memset(frame_scales4[:], 0)

        deal_f_codes(0)
        deal_f_scales(0)
        nc.vector.tensor_copy(
            out=w_rows[:PASSES].rearrange("g t (a e) -> g t a e", e=4),
            in_=w_raw[:].rearrange("g (a t e) -> g t a e", t=SLOTS, e=4),
        )
        for t in range(SLOTS):
            logits(0, t)
        group_targets_vector(0, 0)
        deal_f_codes(1)
        for t in range(SLOTS):
            nc.tensor.transpose(side_bank[:].rearrange("p (g t) -> p t g", t=SLOTS)[:, t, :], w_rows[:, t, :], ident[:])
        nc.vector.tensor_copy(out=w_cols[:], in_=side_bank[:, : PASSES * SLOTS])
        for g in range(1, GROUP_RING):
            group_targets_pool(g)
        for t in range(SLOTS):
            logits(1, t)
        deal_f_scales(1)

        for i in range(STEPS):
            ahead = i + LEAD

            if i < LAG:
                for t in range(SLOTS):
                    logits(ahead, t)
            elif i < INVERT_AT:
                logits_among_intersections(ahead, i - LAG)
            if i == INVERT_AT - 1:
                logits_among_intersections(ahead + 1, i + 1 - LAG)
            if 1 <= i < PASSES:
                group_targets_scalar(i)
            if i == AREAS_FROM:
                predicted_areas(range(0, PASSES // 2))
            if i == AREAS_FROM + 1:
                predicted_areas(range(PASSES // 2, PASSES - 1))
            if i == INVERT_AT:
                predicted_areas([PASSES - 1])
                intersect_step(PASSES - 1)
                for u in range(SLOTS):
                    invert_root(u, side_bank, whole)
                    if u >= 1:
                        square_scalar(u - 1, whole)
                square_scalar(SLOTS - 1, whole)
            if i == INVERT_AT + 1:
                for t in range(LOGIT_BANKS):
                    logits(ahead, t)
            if INVERT_AT + 1 < i and ahead < STEPS:
                logits_among_intersections(ahead, i - 2)
                turn(i - INVERT_AT - 1, side_bank)
                store_rows(0, i - INVERT_AT - 1, side_bank, nc.sync)
            if ahead == STEPS - 1:
                dst, src = y_views(whole)
                nc.scalar.copy(out=dst, in_=src)
            if ahead == STEPS:
                predicted_areas(range(PASSES, i - 2))
            if ahead >= STEPS:
                intersect_step(i - 2)
                predicted_areas([i - 2])

            if i == STEPS - 1:
                quantize(i - 1)
                predicted_areas([i - 1])
                intersect_step(i - 1)
            weigh(i)
            if 1 <= i < PASSES:
                group_targets_vector(i, POOL_RUNS + SCALAR_RUNS)
            if i == 2:
                deal_f_codes(2)
                deal_f_scales(2)
            if i == FRAME_AT:
                group_frame()
            if i == FRAME_AT + 1:
                quantize_frame()
            if i == FRAME_AT + 2:
                spread_frame()
            if 1 <= i < STEPS - 1:
                quantize(i - 1)
            if 1 <= i and i - 1 + GROUP_RING < PASSES:
                group_targets_pool(i - 1 + GROUP_RING)
            if i == INVERT_AT + 1:
                for u in range(SLOTS):
                    ratio(u, whole)
                    intersect(PASSES, u)
                    if u == 1:
                        logits(ahead, SLOTS - 1)
                turn(0, side_bank)
                store_rows(0, 0, side_bank, nc.sync)

        quantize(STEPS - 1)
        predicted_areas([STEPS - 1])
        intersect_step(STEPS - 1)
        quantize_y(0, whole)
        store_codes(0)
        free_banks = [bank for bank in logit_banks if bank is not last_area_bank]
        turn_banks = free_banks + [side_bank, free_banks[0]]
        for cols in (first, second):
            for u in range(SLOTS):
                invert_root(u, last_area_bank, cols)
        for u in range(SLOTS):
            square_vector(u, first)
        for u in range(SLOTS):
            ratio(u, first)
        for u in range(SLOTS):
            square_scalar(u, second)
        for c in (0, 1):
            turn(c, turn_banks[c])
        for c in (0, 1):
            store_rows(1, c, turn_banks[c], nc.sync)
        for u in range(SLOTS):
            ratio(u, second)
        for c in (2, 3):
            turn(c, turn_banks[c])
        for cols in (first, second):
            dst, src = y_views(cols)
            nc.vector.tensor_copy(out=dst, in_=src)
        quantize_y(1, first)
        store_rows(1, 2, turn_banks[2], nc.sync)
        quantize_y(1, second)
        store_codes(1)
        store_rows(1, 3, turn_banks[3], nc.scalar)
        for quadrant in range(QUADRANTS):
            queue = nc.sync if quadrant < QUADRANTS // 2 else nc.scalar
            queue.dma_start(
                out=out_2[0, 4 * quadrant : 4 * quadrant + 4, :].bitcast(I32),
                in_=y_scales[32 * quadrant : 32 * quadrant + 4, :].bitcast(I32),
            )
